import numpy as np
import ml_dtypes


def mxq(x, axis, fmt="e4m3"):
    dtype, down = {"e4m3": (ml_dtypes.float8_e4m3fn, 7), "e5m2": (ml_dtypes.float8_e5m2, 14)}[fmt]
    v = np.moveaxis(np.asarray(x, np.float32).astype(ml_dtypes.bfloat16).astype(np.float64), axis, -1)
    blocks = v.reshape(v.shape[:-1] + (-1, 32))
    amax = np.abs(blocks).max(-1, keepdims=True)
    byte = np.maximum(np.where(amax > 0, np.frexp(amax)[1] - 1 + 127, 0) - down, 1)
    scale = np.exp2(byte - 127.0)
    codes = (blocks / scale).astype(np.float32).astype(dtype).astype(np.float64)
    return np.moveaxis((codes * scale).reshape(v.shape), -1, axis)


WIDE = False


def mx_kscale(k):
    if not WIDE:
        return np.ones(k)
    levels = np.array([10, -10, 5, -5, 0])
    if k % 512:
        return np.exp2(np.random.permutation(np.resize(levels, k // 32))).repeat(32)
    a = np.empty((k // 512, 16))
    for p in range(k // 512):
        a[p, :8] = np.random.permutation(np.resize(levels, 8))
        for g in range(8):
            far = levels[np.abs(levels - a[p, g]) >= 10]
            a[p, g + 8] = far[np.random.randint(len(far))]
    return np.exp2(a.ravel()).repeat(32)


def f64(x):
    return np.asarray(x).astype(np.float64)


def striped(idx):
    return np.tile(idx.reshape(-1, 16).T, (8, 1)).astype(np.uint16)


def unstriped(offs):
    return offs[:16].T.reshape(-1).astype(np.int64)


def striped8(idx):
    return np.concatenate([x.reshape(-1, 16).T for x in idx]).astype(np.uint16)


def runs(offs, k):
    lists = np.stack([offs[16 * r : 16 * r + 16].T.reshape(-1) for r in range(8)]).astype(np.int64)
    return lists[np.arange(k) % 512 // 64]


def pack_weight(w):
    k, n = w.shape
    w = f64(np.asarray(w, np.float32).astype(ml_dtypes.bfloat16)).reshape(k // 32, 32, n)
    amax = np.abs(w).max(1)
    byte = np.clip(np.where(amax > 0, np.frexp(amax)[1] - 1 + 127 - 7, 1), 1, 254)
    scaled = (w * np.exp2(127.0 - byte)[:, None, :]).reshape(k, n).astype(np.float32)
    words = np.ascontiguousarray(scaled.reshape(k // 512, 128, 4, n).transpose(0, 1, 3, 2)).astype(ml_dtypes.float8_e4m3fn).view(np.uint8)
    return words, np.ascontiguousarray(byte.astype(np.uint8).reshape(k // 512, 16, n))


def unpack_weight(words, scales):
    g, p, n, _ = words.shape
    vals = np.ascontiguousarray(words).view(ml_dtypes.float8_e4m3fn).astype(np.float64) * np.repeat(np.exp2(scales.astype(np.float64) - 127.0), 8, axis=1)[..., None]
    return vals.transpose(0, 1, 3, 2).reshape(g * 512, n)


def relu(v):
    return np.maximum(v, 0.0)


K, T, S, V, N, H = 512, 2048, 512, 256, 512, 512


def setup_inputs():
    n = np.random.standard_normal
    s = mx_kscale(K)[:, None]
    u = mx_kscale(H)
    packed_xT = pack_weight(n((K, T)) * s)
    return {
        "x_words": packed_xT[0],
        "x_scales": packed_xT[1],
        "w1": (n((K, H)) / np.sqrt(K) / s * u).astype(np.float32),
        "w2": (n((H, N)) / np.sqrt(H) / u[:, None]).astype(np.float32),
        "offs": striped(np.random.permutation(T)[:S]),
        "src": striped8(np.stack([np.random.permutation(S)[:V] for _ in range(8)])),
        "dst": striped8(np.stack([np.random.permutation(S)[:V] for _ in range(8)])),
    }


def reference(x_words, x_scales, w1, w2, offs, src, dst):
    xq = unpack_weight(x_words, x_scales)[:, unstriped(offs)]
    y = mxq(f64(w1), 0, "e4m3").T @ xq
    m1 = relu(y[np.arange(H)[:, None], runs(src, H)])
    z = y.copy()
    z[np.arange(H)[:, None], runs(dst, H)] = m1
    return mxq(f64(w2), 0, "e4m3").T @ mxq(z, 0, "e4m3")

@@ -1,0 +1,214 @@
+from contextlib import ExitStack
+
+import concourse.mybir as mybir
+
+K, T, S, V, H, N = 512, 2048, 512, 256, 512, 512
+FLOPS = 2 * K * H * S + 2 * H * N * S
+
+F32 = mybir.dt.float32
+BF16 = mybir.dt.bfloat16
+I32 = mybir.dt.int32
+U32 = mybir.dt.uint32
+U16 = mybir.dt.uint16
+U8 = mybir.dt.uint8
+FP8X4 = mybir.dt.float8_e4m3fn_x4
+COPY = mybir.ActivationFunctionType.Copy
+RELU = mybir.ActivationFunctionType.Relu
+
+P = 128
+PACK = 4
+HALF = 256
+LIST_COL = 16
+
+
+def tile_picked_deliver_relu_p_kernel(
+    tc, x_words, x_scales, w1, w2, offs, src, dst, out
+):
+    nc = tc.nc
+    with ExitStack() as ctx:
+        keep = ctx.enter_context(tc.tile_pool(name="keep", bufs=1))
+        psum = ctx.enter_context(tc.psum_pool(name="psum", bufs=8))
+
+        offs_t = keep.tile([P, S // LIST_COL], U16, name="offs_t")
+        src_t = keep.tile([P, V // LIST_COL], U16, name="src_t")
+        dst_t = keep.tile([P, V // LIST_COL], U16, name="dst_t")
+        xw = keep.tile([P, T], U32, name="xw", align_bytes=64)
+        xs = keep.tile([P, T], U8, name="xs", align_bytes=64)
+        w1_raw = keep.tile([P, PACK, H], F32, name="w1_raw", align_bytes=64)
+        w2_raw = keep.tile([P, PACK, N], F32, name="w2_raw", align_bytes=64)
+
+        nc.vector.memset(xs[:].bitcast(I32), 0)
+        nc.sync.dma_start(offs_t[:], offs)
+        w1_rows = w1.rearrange("(p j) c -> p j c", j=PACK)
+        nc.sync.dma_start(out=w1_raw[:, 0:1, :], in_=w1_rows[:, 0:1, :])
+        for q in range(4):
+            nc.sync.dma_start(
+                out=xs[32 * q : 32 * q + 4, :].bitcast(I32),
+                in_=x_scales[0, 4 * q : 4 * q + 4, :].bitcast(I32),
+            )
+        nc.sync.dma_start(out=w1_raw[:, 1:PACK, :], in_=w1_rows[:, 1:PACK, :])
+        nc.sync.dma_start(
+            out=xw[:].bitcast(I32), in_=x_words[0].rearrange("p n t -> p (n t)").bitcast(I32)
+        )
+        nc.sync.dma_start(src_t[:], src)
+        nc.sync.dma_start(dst_t[:], dst)
+        nc.sync.dma_start(out=w2_raw[:], in_=w2.rearrange("(p j) c -> p j c", j=PACK))
+
+        xs_g = keep.tile([P, S], U8, name="xs_g", align_bytes=64)
+
+        nc.vector.tensor_copy(out=xs_g[:], in_=xs[:].indirect(offs_t[:]))
+        w1_cols = w1_raw[:].rearrange("p j (m s e) -> p e m j s", s=2, e=2)
+        w1_codes, w1_scales, w1_bf = {}, {}, {}
+        for e in (1, 0):
+            w1_bf[e] = keep.tile([P, 2, P, PACK], BF16, name="w1_bf%d" % e, align_bytes=64)
+            w1_codes[e] = keep.tile([P, 2 * P], U32, name="w1_codes%d" % e, align_bytes=64)
+            w1_scales[e] = keep.tile([P, 2 * P], U8, name="w1_scales%d" % e, align_bytes=64)
+        nc.vector.tensor_copy(out=w1_bf[1][:].rearrange("p s m j -> p m j s"), in_=w1_cols[:, 1])
+        nc.scalar.activation(w1_bf[0][:].rearrange("p s m j -> p m j s"), w1_cols[:, 0], COPY)
+        for e in (1, 0):
+            nc.vector.quantize_mx(
+                out=w1_codes[e][:].bitcast(FP8X4),
+                scales=w1_scales[e][:],
+                in_=w1_bf[e][:].rearrange("p s m j -> p (s m j)"),
+            )
+
+        xw_g = keep.tile([P, S], U32, name="xw_g", align_bytes=64)
+        for h in range(2):
+            nc.vector.tensor_copy(
+                out=xw_g[:, h * HALF : (h + 1) * HALF],
+                in_=xw[:].indirect(offs_t[:, h * 16 : (h + 1) * 16]),
+            )
+
+        def first_product(t, c0, c1):
+            bank = psum.tile([P, c1 - c0], F32, name="bank", tag="bank")
+            m_cols = slice((t // 2) * P, (t // 2 + 1) * P)
+            nc.tensor.matmul_mx(
+                out=bank[:],
+                lhsT=w1_codes[t % 2][:, m_cols].bitcast(FP8X4),
+                lhsT_scale=w1_scales[t % 2][:, m_cols],
+                rhs=xw_g[:, c0:c1].bitcast(FP8X4),
+                rhs_scale=xs_g[:, c0:c1],
+                start=True,
+                stop=True,
+            )
+            return bank
+
+        z = {}
+        for t in (1, 3):
+            z[t] = keep.tile([P, S], F32, name="z%d" % t, align_bytes=64)
+        for t in (0, 2):
+            z[t] = keep.tile([P, 2 * S], F32, name="z%d" % t, align_bytes=64)
+        got, act = {}, {}
+        for t in range(PACK):
+            got[t] = keep.tile([P, V], F32, name="got%d" % t, align_bytes=64)
+            act[t] = keep.tile([P, V], F32, name="act%d" % t, tag="act%d" % t, align_bytes=64)
+
+        y1a = first_product(1, 0, HALF)
+        y1b = first_product(1, HALF, S)
+        y3 = first_product(3, 0, S)
+        y0 = first_product(0, 0, S)
+        y2 = first_product(2, 0, S)
+
+        def fetch(t):
+            nc.vector.tensor_copy(out=got[t][:], in_=z[t][:].indirect(src_t[:]))
+
+        def activate(t):
+            nc.scalar.activation(act[t][:], got[t][:], RELU)
+
+        def deliver(t):
+            nc.vector.tensor_copy(out=z[t][:].indirect(dst_t[:]), in_=act[t][:])
+
+        def join(t):
+            nc.scalar.copy(z[t - 1][:, S : 2 * S], z[t][:])
+
+        w2_bf = [keep.tile([P, P, PACK], BF16, name="w2_bf%d" % mt, align_bytes=64) for mt in range(4)]
+        w2_scales = keep.tile([P, N], U8, name="w2_scales", align_bytes=64)
+
+        def round_w2(mt):
+            nc.scalar.copy(
+                w2_bf[mt][:].rearrange("p (c i) j -> p c j i", i=4),
+                w2_raw[:, :, mt * P : (mt + 1) * P].rearrange("p j (c i) -> p c j i", i=4),
+            )
+
+        def quantize_w2(mt, codes):
+            nc.vector.quantize_mx(
+                out=codes.bitcast(FP8X4),
+                scales=w2_scales[:, mt * P : (mt + 1) * P],
+                in_=w2_bf[mt][:].rearrange("p n j -> p (n j)"),
+            )
+
+        def quantize_z(c):
+            nc.vector.quantize_mx(
+                out=z_codes[c][:].bitcast(FP8X4),
+                scales=z_scales[c][:],
+                in_=z_bf[c][:].rearrange("p n j -> p (n j)"),
+            )
+
+        z_bf = [keep.tile([P, HALF, PACK], BF16, name="z_bf%d" % c, align_bytes=64) for c in range(2)]
+        z_codes = [keep.tile([P, HALF], U32, name="z_codes%d" % c, align_bytes=64) for c in range(2)]
+        z_scales = [keep.tile([P, HALF], U8, name="z_scales%d" % c, align_bytes=64) for c in range(2)]
+
+        def pair_views(t, c):
+            pair = z[t][:].rearrange("p (s n) -> p n s", s=2)
+            return z_bf[c][:, :, t : t + 2], pair[:, c * HALF : (c + 1) * HALF, :]
+
+        nc.scalar.copy(z[1][:, 0:HALF], y1a[:])
+        nc.scalar.copy(z[1][:, HALF:S], y1b[:])
+        nc.scalar.copy(z[3][:], y3[:])
+        fetch(1)
+        fetch(3)
+        activate(1)
+        activate(3)
+        deliver(1)
+        deliver(3)
+        nc.scalar.copy(z[0][:, 0:S], y0[:])
+        round_w2(0)
+        join(1)
+        nc.scalar.copy(z[2][:, 0:S], y2[:])
+        round_w2(1)
+        join(3)
+        fetch(0)
+        activate(0)
+        w2_first = keep.tile([P, P], U32, name="w2_first", tag="act3", align_bytes=64)
+        quantize_w2(0, w2_first[:])
+        fetch(2)
+        activate(2)
+        deliver(0)
+        round_w2(2)
+        round_w2(3)
+        deliver(2)
+        for c in range(2):
+            nc.scalar.copy(*pair_views(0, c))
+        w2_rest = keep.tile([P, 3 * P], U32, name="w2_rest", tag="act2", align_bytes=64)
+        w2_codes = [w2_first[:]] + [w2_rest[:, i * P : (i + 1) * P] for i in range(3)]
+        nc.vector.tensor_copy(*pair_views(2, 0))
+        nc.scalar.copy(*pair_views(2, 1))
+        quantize_w2(1, w2_codes[1])
+        quantize_z(0)
+        quantize_w2(2, w2_codes[2])
+        quantize_w2(3, w2_codes[3])
+        quantize_z(1)
+
+        out_rows = out.rearrange("(mt p) j -> p mt j", p=P)
+        for c in range(2):
+            for u in range(2):
+                res = keep.tile([P, 2, HALF], F32, name="res%d%d" % (c, u), align_bytes=64)
+                for i in range(2):
+                    m_cols = slice((2 * u + i) * P, (2 * u + i + 1) * P)
+                    bank = psum.tile([P, HALF], F32, name="bank", tag="bank")
+                    nc.tensor.matmul_mx(
+                        out=bank[:],
+                        lhsT=w2_codes[2 * u + i].bitcast(FP8X4),
+                        lhsT_scale=w2_scales[:, m_cols],
+                        rhs=z_codes[c][:].bitcast(FP8X4),
+                        rhs_scale=z_scales[c][:],
+                        start=True,
+                        stop=True,
+                    )
+                    if i == 0:
+                        nc.scalar.copy(res[:, i, :], bank[:])
+                    else:
+                        nc.vector.tensor_copy(out=res[:, i, :], in_=bank[:])
+                nc.sync.dma_start(
+                    out=out_rows[:, 2 * u : 2 * u + 2, c * HALF : (c + 1) * HALF], in_=res[:]
+                )

@@ -34,19 +34,19 @@ def tile_picked_deliver_relu_p_kernel(
         dst_t = keep.tile([P, V // LIST_COL], U16, name="dst_t")
         xw = keep.tile([P, T], U32, name="xw", align_bytes=64)
         xs = keep.tile([P, T], U8, name="xs", align_bytes=64)
-        w1_raw = keep.tile([P, PACK, H], F32, name="w1_raw", align_bytes=64)
+        w1_raw = [keep.tile([P, 2, H], F32, name="w1_raw%d" % u, align_bytes=64) for u in range(2)]
         w2_raw = keep.tile([P, PACK, N], F32, name="w2_raw", align_bytes=64)
 
         nc.vector.memset(xs[:].bitcast(I32), 0)
-        nc.sync.dma_start(offs_t[:], offs)
         w1_rows = w1.rearrange("(p j) c -> p j c", j=PACK)
-        nc.sync.dma_start(out=w1_raw[:, 0:1, :], in_=w1_rows[:, 0:1, :])
+        nc.sync.dma_start(out=w1_raw[0][:], in_=w1_rows[:, 0:2, :])
+        nc.sync.dma_start(offs_t[:], offs)
         for q in range(4):
             nc.sync.dma_start(
                 out=xs[32 * q : 32 * q + 4, :].bitcast(I32),
                 in_=x_scales[0, 4 * q : 4 * q + 4, :].bitcast(I32),
             )
-        nc.sync.dma_start(out=w1_raw[:, 1:PACK, :], in_=w1_rows[:, 1:PACK, :])
+        nc.sync.dma_start(out=w1_raw[1][:], in_=w1_rows[:, 2:PACK, :])
         nc.sync.dma_start(
             out=xw[:].bitcast(I32), in_=x_words[0].rearrange("p n t -> p (n t)").bitcast(I32)
         )
@@ -56,15 +56,21 @@ def tile_picked_deliver_relu_p_kernel(
 
         xs_g = keep.tile([P, S], U8, name="xs_g", align_bytes=64)
 
-        nc.vector.tensor_copy(out=xs_g[:], in_=xs[:].indirect(offs_t[:]))
-        w1_cols = w1_raw[:].rearrange("p j (m s e) -> p e m j s", s=2, e=2)
         w1_codes, w1_scales, w1_bf = {}, {}, {}
         for e in (1, 0):
             w1_bf[e] = keep.tile([P, 2, P, PACK], BF16, name="w1_bf%d" % e, align_bytes=64)
             w1_codes[e] = keep.tile([P, 2 * P], U32, name="w1_codes%d" % e, align_bytes=64)
             w1_scales[e] = keep.tile([P, 2 * P], U8, name="w1_scales%d" % e, align_bytes=64)
-        nc.vector.tensor_copy(out=w1_bf[1][:].rearrange("p s m j -> p m j s"), in_=w1_cols[:, 1])
-        nc.scalar.activation(w1_bf[0][:].rearrange("p s m j -> p m j s"), w1_cols[:, 0], COPY)
+
+        def w1_views(e, u):
+            cols = w1_raw[u][:].rearrange("p j (m s e) -> p e m j s", s=2, e=2)
+            return w1_bf[e][:, :, :, 2 * u : 2 * u + 2].rearrange("p s m j -> p m j s"), cols[:, e]
+
+        nc.vector.tensor_copy(*w1_views(1, 0))
+        nc.scalar.activation(*w1_views(0, 0), COPY)
+        nc.vector.tensor_copy(out=xs_g[:], in_=xs[:].indirect(offs_t[:]))
+        nc.vector.tensor_copy(*w1_views(1, 1))
+        nc.scalar.activation(*w1_views(0, 1), COPY)
         for e in (1, 0):
             nc.vector.quantize_mx(
                 out=w1_codes[e][:].bitcast(FP8X4),
@@ -103,9 +109,10 @@ def tile_picked_deliver_relu_p_kernel(
             got[t] = keep.tile([P, V], F32, name="got%d" % t, align_bytes=64)
             act[t] = keep.tile([P, V], F32, name="act%d" % t, tag="act%d" % t, align_bytes=64)
 
-        y1a = first_product(1, 0, HALF)
-        y1b = first_product(1, HALF, S)
-        y3 = first_product(3, 0, S)
+        for t in (0, 2):
+            nc.vector.memset(z[t][:, S : 2 * S], 0.0)
+
+        early = [(t, h, first_product(t, h * HALF, (h + 1) * HALF)) for h in range(2) for t in (1, 3)]
         y0 = first_product(0, 0, S)
         y2 = first_product(2, 0, S)
 
@@ -130,85 +137,94 @@ def tile_picked_deliver_relu_p_kernel(
                 w2_raw[:, :, mt * P : (mt + 1) * P].rearrange("p j (c i) -> p c j i", i=4),
             )
 
-        def quantize_w2(mt, codes):
+        def quantize_w2(mt):
             nc.vector.quantize_mx(
-                out=codes.bitcast(FP8X4),
+                out=w2_codes[:, mt * P : (mt + 1) * P].bitcast(FP8X4),
                 scales=w2_scales[:, mt * P : (mt + 1) * P],
                 in_=w2_bf[mt][:].rearrange("p n j -> p (n j)"),
             )
 
         def quantize_z(c):
             nc.vector.quantize_mx(
-                out=z_codes[c][:].bitcast(FP8X4),
-                scales=z_scales[c][:],
+                out=z_codes[:, c * HALF : (c + 1) * HALF].bitcast(FP8X4),
+                scales=z_scales[:, c * HALF : (c + 1) * HALF],
                 in_=z_bf[c][:].rearrange("p n j -> p (n j)"),
             )
 
         z_bf = [keep.tile([P, HALF, PACK], BF16, name="z_bf%d" % c, align_bytes=64) for c in range(2)]
-        z_codes = [keep.tile([P, HALF], U32, name="z_codes%d" % c, align_bytes=64) for c in range(2)]
-        z_scales = [keep.tile([P, HALF], U8, name="z_scales%d" % c, align_bytes=64) for c in range(2)]
+        z_codes = keep.tile([P, S], U32, name="z_codes", align_bytes=64)
+        z_scales = keep.tile([P, S], U8, name="z_scales", align_bytes=64)
 
         def pair_views(t, c):
             pair = z[t][:].rearrange("p (s n) -> p n s", s=2)
             return z_bf[c][:, :, t : t + 2], pair[:, c * HALF : (c + 1) * HALF, :]
 
-        nc.scalar.copy(z[1][:, 0:HALF], y1a[:])
-        nc.scalar.copy(z[1][:, HALF:S], y1b[:])
-        nc.scalar.copy(z[3][:], y3[:])
+        for t, h, bank in early:
+            nc.scalar.copy(z[t][:, h * HALF : (h + 1) * HALF], bank[:])
         fetch(1)
         fetch(3)
         activate(1)
-        activate(3)
         deliver(1)
-        deliver(3)
         nc.scalar.copy(z[0][:, 0:S], y0[:])
-        round_w2(0)
-        join(1)
-        nc.scalar.copy(z[2][:, 0:S], y2[:])
-        round_w2(1)
-        join(3)
         fetch(0)
-        activate(0)
-        w2_first = keep.tile([P, P], U32, name="w2_first", tag="act3", align_bytes=64)
-        quantize_w2(0, w2_first[:])
+        activate(3)
+        deliver(3)
+        nc.scalar.copy(z[2][:, 0:S], y2[:])
         fetch(2)
-        activate(2)
+        round_w2(0)
+        round_w2(1)
+        activate(0)
+        join(1)
         deliver(0)
         round_w2(2)
         round_w2(3)
+        activate(2)
+        join(3)
         deliver(2)
         for c in range(2):
             nc.scalar.copy(*pair_views(0, c))
-        w2_rest = keep.tile([P, 3 * P], U32, name="w2_rest", tag="act2", align_bytes=64)
-        w2_codes = [w2_first[:]] + [w2_rest[:, i * P : (i + 1) * P] for i in range(3)]
+        w2_codes = keep.tile([P, N], U32, name="w2_codes", tag="act2", align_bytes=64)
         nc.vector.tensor_copy(*pair_views(2, 0))
         nc.scalar.copy(*pair_views(2, 1))
-        quantize_w2(1, w2_codes[1])
+        quantize_w2(0)
         quantize_z(0)
-        quantize_w2(2, w2_codes[2])
-        quantize_w2(3, w2_codes[3])
+        quantize_w2(1)
         quantize_z(1)
+        quantize_w2(2)
+        quantize_w2(3)
+
+        def second_product(mt, c, res, on_vector):
+            m_cols = slice(mt * P, (mt + 1) * P)
+            tokens = slice(c * HALF, (c + 1) * HALF)
+            bank = psum.tile([P, HALF], F32, name="bank", tag="bank")
+            nc.tensor.matmul_mx(
+                out=bank[:],
+                lhsT=w2_codes[:, m_cols].bitcast(FP8X4),
+                lhsT_scale=w2_scales[:, m_cols],
+                rhs=z_codes[:, tokens].bitcast(FP8X4),
+                rhs_scale=z_scales[:, tokens],
+                start=True,
+                stop=True,
+            )
+            if on_vector:
+                nc.vector.tensor_copy(out=res, in_=bank[:])
+            else:
+                nc.scalar.copy(res, bank[:])
 
         out_rows = out.rearrange("(mt p) j -> p mt j", p=P)
+        for mt in range(2):
+            res = keep.tile([P, HALF], F32, name="res_a%d" % mt, align_bytes=64)
+            second_product(mt, 0, res[:], False)
+            nc.sync.dma_start(out=out_rows[:, mt, 0:HALF], in_=res[:])
+        res = keep.tile([P, 2, HALF], F32, name="res_b", align_bytes=64)
+        for mt in range(2):
+            second_product(mt, 1, res[:, mt, :], mt == 1)
+        nc.sync.dma_start(out=out_rows[:, 0:2, HALF:S], in_=res[:])
+        res = keep.tile([P, S], F32, name="res_c", align_bytes=64)
         for c in range(2):
-            for u in range(2):
-                res = keep.tile([P, 2, HALF], F32, name="res%d%d" % (c, u), align_bytes=64)
-                for i in range(2):
-                    m_cols = slice((2 * u + i) * P, (2 * u + i + 1) * P)
-                    bank = psum.tile([P, HALF], F32, name="bank", tag="bank")
-                    nc.tensor.matmul_mx(
-                        out=bank[:],
-                        lhsT=w2_codes[2 * u + i].bitcast(FP8X4),
-                        lhsT_scale=w2_scales[:, m_cols],
-                        rhs=z_codes[c][:].bitcast(FP8X4),
-                        rhs_scale=z_scales[c][:],
-                        start=True,
-                        stop=True,
-                    )
-                    if i == 0:
-                        nc.scalar.copy(res[:, i, :], bank[:])
-                    else:
-                        nc.vector.tensor_copy(out=res[:, i, :], in_=bank[:])
-                nc.sync.dma_start(
-                    out=out_rows[:, 2 * u : 2 * u + 2, c * HALF : (c + 1) * HALF], in_=res[:]
-                )
+            second_product(2, c, res[:, c * HALF : (c + 1) * HALF], c == 1)
+        nc.sync.dma_start(out=out_rows[:, 2, :], in_=res[:])
+        for c in range(2):
+            res = keep.tile([P, HALF], F32, name="res_d%d" % c, align_bytes=64)
+            second_product(3, c, res[:], c == 1)
+            nc.sync.dma_start(out=out_rows[:, 3, c * HALF : (c + 1) * HALF], in_=res[:])

@@ -46,10 +46,10 @@ def tile_picked_deliver_relu_p_kernel(
                 out=xs[32 * q : 32 * q + 4, :].bitcast(I32),
                 in_=x_scales[0, 4 * q : 4 * q + 4, :].bitcast(I32),
             )
-        nc.sync.dma_start(out=w1_raw[1][:], in_=w1_rows[:, 2:PACK, :])
         nc.sync.dma_start(
             out=xw[:].bitcast(I32), in_=x_words[0].rearrange("p n t -> p (n t)").bitcast(I32)
         )
+        nc.sync.dma_start(out=w1_raw[1][:], in_=w1_rows[:, 2:PACK, :])
         nc.sync.dma_start(src_t[:], src)
         nc.sync.dma_start(dst_t[:], dst)
         nc.sync.dma_start(out=w2_raw[:], in_=w2.rearrange("(p j) c -> p j c", j=PACK))
@@ -66,24 +66,25 @@ def tile_picked_deliver_relu_p_kernel(
             cols = w1_raw[u][:].rearrange("p j (m s e) -> p e m j s", s=2, e=2)
             return w1_bf[e][:, :, :, 2 * u : 2 * u + 2].rearrange("p s m j -> p m j s"), cols[:, e]
 
-        nc.vector.tensor_copy(*w1_views(1, 0))
-        nc.scalar.activation(*w1_views(0, 0), COPY)
-        nc.vector.tensor_copy(out=xs_g[:], in_=xs[:].indirect(offs_t[:]))
-        nc.vector.tensor_copy(*w1_views(1, 1))
-        nc.scalar.activation(*w1_views(0, 1), COPY)
-        for e in (1, 0):
+        def quantize_w1(e, s0, s1):
             nc.vector.quantize_mx(
-                out=w1_codes[e][:].bitcast(FP8X4),
-                scales=w1_scales[e][:],
-                in_=w1_bf[e][:].rearrange("p s m j -> p (s m j)"),
+                out=w1_codes[e][:, s0 * P : s1 * P].bitcast(FP8X4),
+                scales=w1_scales[e][:, s0 * P : s1 * P],
+                in_=w1_bf[e][:, s0:s1].rearrange("p s m j -> p (s m j)"),
             )
 
         xw_g = keep.tile([P, S], U32, name="xw_g", align_bytes=64)
-        for h in range(2):
-            nc.vector.tensor_copy(
-                out=xw_g[:, h * HALF : (h + 1) * HALF],
-                in_=xw[:].indirect(offs_t[:, h * 16 : (h + 1) * 16]),
-            )
+        nc.vector.tensor_copy(*w1_views(1, 0))
+        nc.scalar.activation(*w1_views(0, 0), COPY)
+        nc.vector.tensor_copy(out=xs_g[:], in_=xs[:].indirect(offs_t[:]))
+        nc.vector.tensor_copy(out=xw_g[:], in_=xw[:].indirect(offs_t[:]))
+        late_out, late_in = w1_views(1, 1)
+        for s in range(2):
+            nc.vector.tensor_copy(late_out[:, :, :, s], late_in[:, :, :, s])
+        nc.scalar.activation(*w1_views(0, 1), COPY)
+        quantize_w1(1, 0, 1)
+        quantize_w1(1, 1, 2)
+        quantize_w1(0, 0, 2)
 
         def first_product(t, c0, c1):
             bank = psum.tile([P, c1 - c0], F32, name="bank", tag="bank")
@@ -112,7 +113,7 @@ def tile_picked_deliver_relu_p_kernel(
         for t in (0, 2):
             nc.vector.memset(z[t][:, S : 2 * S], 0.0)
 
-        early = [(t, h, first_product(t, h * HALF, (h + 1) * HALF)) for h in range(2) for t in (1, 3)]
+        early = [(t, h, first_product(t, h * HALF, (h + 1) * HALF)) for t in (1, 3) for h in range(2)]
         y0 = first_product(0, 0, S)
         y2 = first_product(2, 0, S)
 
@@ -128,36 +129,45 @@ def tile_picked_deliver_relu_p_kernel(
         def join(t):
             nc.scalar.copy(z[t - 1][:, S : 2 * S], z[t][:])
 
-        w2_bf = [keep.tile([P, P, PACK], BF16, name="w2_bf%d" % mt, align_bytes=64) for mt in range(4)]
+        w2_bf = [keep.tile([P, HALF, PACK], BF16, name="w2_bf%d" % u, align_bytes=64) for u in range(2)]
         w2_scales = keep.tile([P, N], U8, name="w2_scales", align_bytes=64)
+        w2_codes = {}
 
         def round_w2(mt):
+            lo = (mt % 2) * P
             nc.scalar.copy(
-                w2_bf[mt][:].rearrange("p (c i) j -> p c j i", i=4),
+                w2_bf[mt // 2][:, lo : lo + P, :].rearrange("p (c i) j -> p c j i", i=4),
                 w2_raw[:, :, mt * P : (mt + 1) * P].rearrange("p j (c i) -> p c j i", i=4),
             )
 
-        def quantize_w2(mt):
+        def quantize_w2(u, slot):
+            w2_codes[u] = keep.tile([P, HALF], U32, name="w2_codes%d" % u, tag=slot, align_bytes=64)
             nc.vector.quantize_mx(
-                out=w2_codes[:, mt * P : (mt + 1) * P].bitcast(FP8X4),
-                scales=w2_scales[:, mt * P : (mt + 1) * P],
-                in_=w2_bf[mt][:].rearrange("p n j -> p (n j)"),
+                out=w2_codes[u][:].bitcast(FP8X4),
+                scales=w2_scales[:, u * HALF : (u + 1) * HALF],
+                in_=w2_bf[u][:].rearrange("p n j -> p (n j)"),
             )
 
-        def quantize_z(c):
-            nc.vector.quantize_mx(
-                out=z_codes[:, c * HALF : (c + 1) * HALF].bitcast(FP8X4),
-                scales=z_scales[:, c * HALF : (c + 1) * HALF],
-                in_=z_bf[c][:].rearrange("p n j -> p (n j)"),
-            )
-
-        z_bf = [keep.tile([P, HALF, PACK], BF16, name="z_bf%d" % c, align_bytes=64) for c in range(2)]
+        chunks = ((0, P), (P, HALF), (HALF, S))
+        z_bf = [
+            keep.tile([P, j1 - j0, PACK], BF16, name="z_bf%d" % c, tag="z_bf%d" % c, align_bytes=64)
+            for c, (j0, j1) in enumerate(chunks)
+        ]
         z_codes = keep.tile([P, S], U32, name="z_codes", align_bytes=64)
         z_scales = keep.tile([P, S], U8, name="z_scales", align_bytes=64)
 
+        def quantize_z(c):
+            j0, j1 = chunks[c]
+            nc.vector.quantize_mx(
+                out=z_codes[:, j0:j1].bitcast(FP8X4),
+                scales=z_scales[:, j0:j1],
+                in_=z_bf[c][:].rearrange("p n j -> p (n j)"),
+            )
+
         def pair_views(t, c):
+            j0, j1 = chunks[c]
             pair = z[t][:].rearrange("p (s n) -> p n s", s=2)
-            return z_bf[c][:, :, t : t + 2], pair[:, c * HALF : (c + 1) * HALF, :]
+            return z_bf[c][:, :, t : t + 2], pair[:, j0:j1, :]
 
         for t, h, bank in early:
             nc.scalar.copy(z[t][:, h * HALF : (h + 1) * HALF], bank[:])
@@ -177,54 +187,49 @@ def tile_picked_deliver_relu_p_kernel(
         join(1)
         deliver(0)
         round_w2(2)
-        round_w2(3)
         activate(2)
         join(3)
+        round_w2(3)
         deliver(2)
-        for c in range(2):
+        for c in range(3):
             nc.scalar.copy(*pair_views(0, c))
-        w2_codes = keep.tile([P, N], U32, name="w2_codes", tag="act2", align_bytes=64)
-        nc.vector.tensor_copy(*pair_views(2, 0))
-        nc.scalar.copy(*pair_views(2, 1))
-        quantize_w2(0)
-        quantize_z(0)
-        quantize_w2(1)
-        quantize_z(1)
-        quantize_w2(2)
-        quantize_w2(3)
 
-        def second_product(mt, c, res, on_vector):
+        def second_product(mt, j0, j1, dest):
             m_cols = slice(mt * P, (mt + 1) * P)
-            tokens = slice(c * HALF, (c + 1) * HALF)
-            bank = psum.tile([P, HALF], F32, name="bank", tag="bank")
             nc.tensor.matmul_mx(
-                out=bank[:],
-                lhsT=w2_codes[:, m_cols].bitcast(FP8X4),
+                out=dest,
+                lhsT=w2_codes[mt // 2][:, (mt % 2) * P : (mt % 2 + 1) * P].bitcast(FP8X4),
                 lhsT_scale=w2_scales[:, m_cols],
-                rhs=z_codes[:, tokens].bitcast(FP8X4),
-                rhs_scale=z_scales[:, tokens],
+                rhs=z_codes[:, j0:j1].bitcast(FP8X4),
+                rhs_scale=z_scales[:, j0:j1],
                 start=True,
                 stop=True,
             )
-            if on_vector:
-                nc.vector.tensor_copy(out=res, in_=bank[:])
-            else:
-                nc.scalar.copy(res, bank[:])
 
         out_rows = out.rearrange("(mt p) j -> p mt j", p=P)
-        for mt in range(2):
-            res = keep.tile([P, HALF], F32, name="res_a%d" % mt, align_bytes=64)
-            second_product(mt, 0, res[:], False)
-            nc.sync.dma_start(out=out_rows[:, mt, 0:HALF], in_=res[:])
-        res = keep.tile([P, 2, HALF], F32, name="res_b", align_bytes=64)
-        for mt in range(2):
-            second_product(mt, 1, res[:, mt, :], mt == 1)
-        nc.sync.dma_start(out=out_rows[:, 0:2, HALF:S], in_=res[:])
-        res = keep.tile([P, S], F32, name="res_c", align_bytes=64)
-        for c in range(2):
-            second_product(2, c, res[:, c * HALF : (c + 1) * HALF], c == 1)
-        nc.sync.dma_start(out=out_rows[:, 2, :], in_=res[:])
-        for c in range(2):
-            res = keep.tile([P, HALF], F32, name="res_d%d" % c, align_bytes=64)
-            second_product(3, c, res[:], c == 1)
-            nc.sync.dma_start(out=out_rows[:, 3, c * HALF : (c + 1) * HALF], in_=res[:])
+
+        def output_piece(mt0, mt1, j0, j1, on_vector):
+            bank = psum.tile([P, mt1 - mt0, j1 - j0], F32, name="bank", tag="bank")
+            for mt in range(mt0, mt1):
+                second_product(mt, j0, j1, bank[:, mt - mt0, :])
+            res = keep.tile([P, mt1 - mt0, j1 - j0], F32, name="res%d_%d" % (mt0, j0), align_bytes=64)
+            if on_vector:
+                nc.vector.tensor_copy(out=res[:], in_=bank[:])
+            else:
+                nc.scalar.copy(res[:], bank[:])
+            nc.sync.dma_start(out=out_rows[:, mt0:mt1, j0:j1], in_=res[:])
+
+        nc.vector.tensor_copy(*pair_views(2, 0))
+        nc.scalar.copy(*pair_views(2, 1))
+        nc.scalar.copy(*pair_views(2, 2))
+        quantize_w2(0, "act2")
+        quantize_z(0)
+        quantize_z(1)
+        quantize_w2(1, "z_bf1")
+        quantize_z(2)
+        output_piece(0, 2, 0, P, False)
+        output_piece(0, 2, P, HALF, False)
+        output_piece(2, 3, 0, HALF, True)
+        output_piece(3, 4, 0, HALF, False)
+        for mt in range(4):
+            output_piece(mt, mt + 1, HALF, S, mt % 2 == 0)

@@ -32,27 +32,21 @@ def tile_picked_deliver_relu_p_kernel(
         offs_t = keep.tile([P, S // LIST_COL], U16, name="offs_t")
         src_t = keep.tile([P, V // LIST_COL], U16, name="src_t")
         dst_t = keep.tile([P, V // LIST_COL], U16, name="dst_t")
-        xw = keep.tile([P, T], U32, name="xw", align_bytes=64)
+        xw = keep.tile([P, T], U32, name="xw", tag="xw", align_bytes=64)
         xs = keep.tile([P, T], U8, name="xs", align_bytes=64)
         w1_raw = [keep.tile([P, 2, H], F32, name="w1_raw%d" % u, align_bytes=64) for u in range(2)]
-        w2_raw = keep.tile([P, PACK, N], F32, name="w2_raw", align_bytes=64)
 
         nc.vector.memset(xs[:].bitcast(I32), 0)
         w1_rows = w1.rearrange("(p j) c -> p j c", j=PACK)
-        nc.sync.dma_start(out=w1_raw[0][:], in_=w1_rows[:, 0:2, :])
+        x_cols = x_words[0].rearrange("p n t -> p (n t)").bitcast(I32)
+        nc.sync.dma_start(out=xw[:, 0 : T // 4].bitcast(I32), in_=x_cols[:, 0 : T // 4])
         nc.sync.dma_start(offs_t[:], offs)
-        for q in range(4):
-            nc.sync.dma_start(
-                out=xs[32 * q : 32 * q + 4, :].bitcast(I32),
-                in_=x_scales[0, 4 * q : 4 * q + 4, :].bitcast(I32),
-            )
-        nc.sync.dma_start(
-            out=xw[:].bitcast(I32), in_=x_words[0].rearrange("p n t -> p (n t)").bitcast(I32)
-        )
+        nc.sync.dma_start(out=xs[0:P:8, :].bitcast(I32), in_=x_scales[0].bitcast(I32))
+        nc.sync.dma_start(out=xw[:, T // 4 : T].bitcast(I32), in_=x_cols[:, T // 4 : T])
+        nc.sync.dma_start(out=w1_raw[0][:], in_=w1_rows[:, 0:2, :])
         nc.sync.dma_start(out=w1_raw[1][:], in_=w1_rows[:, 2:PACK, :])
         nc.sync.dma_start(src_t[:], src)
         nc.sync.dma_start(dst_t[:], dst)
-        nc.sync.dma_start(out=w2_raw[:], in_=w2.rearrange("(p j) c -> p j c", j=PACK))
 
         xs_g = keep.tile([P, S], U8, name="xs_g", align_bytes=64)
 
@@ -74,10 +68,16 @@ def tile_picked_deliver_relu_p_kernel(
             )
 
         xw_g = keep.tile([P, S], U32, name="xw_g", align_bytes=64)
+        xs_spread = keep.tile([P, S], U8, name="xs_spread", align_bytes=64)
+        nc.vector.tensor_copy(out=xs_spread[:], in_=xs[:].indirect(offs_t[:]))
+        nc.vector.tensor_copy(out=xs_g[:].bitcast(I32), in_=xs_spread[:].bitcast(I32))
+        for r in range(1, 4):
+            nc.sync.dma_start(out=xs_g[r:P:32, :].bitcast(I32), in_=xs_spread[8 * r : P : 32, :].bitcast(I32))
+        nc.vector.tensor_copy(out=xw_g[:], in_=xw[:].indirect(offs_t[:]))
+        w2_raw = keep.tile([P, PACK, N], F32, name="w2_raw", tag="xw", align_bytes=64)
+        nc.sync.dma_start(out=w2_raw[:], in_=w2.rearrange("(p j) c -> p j c", j=PACK))
         nc.vector.tensor_copy(*w1_views(1, 0))
         nc.scalar.activation(*w1_views(0, 0), COPY)
-        nc.vector.tensor_copy(out=xs_g[:], in_=xs[:].indirect(offs_t[:]))
-        nc.vector.tensor_copy(out=xw_g[:], in_=xw[:].indirect(offs_t[:]))
         late_out, late_in = w1_views(1, 1)
         for s in range(2):
             nc.vector.tensor_copy(late_out[:, :, :, s], late_in[:, :, :, s])
@@ -113,7 +113,8 @@ def tile_picked_deliver_relu_p_kernel(
         for t in (0, 2):
             nc.vector.memset(z[t][:, S : 2 * S], 0.0)
 
-        early = [(t, h, first_product(t, h * HALF, (h + 1) * HALF)) for t in (1, 3) for h in range(2)]
+        y1 = [first_product(1, q * P, (q + 1) * P) for q in range(4)]
+        y3 = [first_product(3, h * HALF, (h + 1) * HALF) for h in range(2)]
         y0 = first_product(0, 0, S)
         y2 = first_product(2, 0, S)
 
@@ -169,9 +170,14 @@ def tile_picked_deliver_relu_p_kernel(
             pair = z[t][:].rearrange("p (s n) -> p n s", s=2)
             return z_bf[c][:, :, t : t + 2], pair[:, j0:j1, :]
 
-        for t, h, bank in early:
-            nc.scalar.copy(z[t][:, h * HALF : (h + 1) * HALF], bank[:])
+        for q, bank in enumerate(y1):
+            if q % 2 == 0:
+                nc.scalar.copy(z[1][:, q * P : (q + 1) * P], bank[:])
+            else:
+                nc.vector.tensor_copy(z[1][:, q * P : (q + 1) * P], bank[:])
         fetch(1)
+        for h, bank in enumerate(y3):
+            nc.scalar.copy(z[3][:, h * HALF : (h + 1) * HALF], bank[:])
         fetch(3)
         activate(1)
         deliver(1)

@@ -113,10 +113,18 @@ def tile_picked_deliver_relu_p_kernel(
         for t in (0, 2):
             nc.vector.memset(z[t][:, S : 2 * S], 0.0)
 
-        y1 = [first_product(1, q * P, (q + 1) * P) for q in range(4)]
-        y3 = [first_product(3, h * HALF, (h + 1) * HALF) for h in range(2)]
-        y0 = first_product(0, 0, S)
-        y2 = first_product(2, 0, S)
+        warm = psum.tile([P, S], F32, name="warm", tag="bank")
+        for u in range(2):
+            nc.tensor.matmul_mx(
+                out=warm[:],
+                lhsT=xw_g[:, 0:P].bitcast(FP8X4),
+                lhsT_scale=xs_spread[:, 0:P],
+                rhs=xw_g[:].bitcast(FP8X4),
+                rhs_scale=xs_spread[:],
+                start=True,
+                stop=True,
+            )
+        early = [(t, q, first_product(t, q * P, (q + 1) * P)) for t in (1, 3) for q in range(4)]
 
         def fetch(t):
             nc.vector.tensor_copy(out=got[t][:], in_=z[t][:].indirect(src_t[:]))
@@ -170,22 +178,20 @@ def tile_picked_deliver_relu_p_kernel(
             pair = z[t][:].rearrange("p (s n) -> p n s", s=2)
             return z_bf[c][:, :, t : t + 2], pair[:, j0:j1, :]
 
-        for q, bank in enumerate(y1):
-            if q % 2 == 0:
-                nc.scalar.copy(z[1][:, q * P : (q + 1) * P], bank[:])
+        for t, q, bank in early:
+            if (t, q) in ((1, 1), (1, 3), (3, 0)):
+                nc.vector.tensor_copy(z[t][:, q * P : (q + 1) * P], bank[:])
             else:
-                nc.vector.tensor_copy(z[1][:, q * P : (q + 1) * P], bank[:])
+                nc.scalar.copy(z[t][:, q * P : (q + 1) * P], bank[:])
         fetch(1)
-        for h, bank in enumerate(y3):
-            nc.scalar.copy(z[3][:, h * HALF : (h + 1) * HALF], bank[:])
         fetch(3)
         activate(1)
         deliver(1)
-        nc.scalar.copy(z[0][:, 0:S], y0[:])
+        nc.scalar.copy(z[0][:, 0:S], first_product(0, 0, S)[:])
         fetch(0)
         activate(3)
         deliver(3)
-        nc.scalar.copy(z[2][:, 0:S], y2[:])
+        nc.scalar.copy(z[2][:, 0:S], first_product(2, 0, S)[:])
         fetch(2)
         round_w2(0)
         round_w2(1)

@@ -107,8 +107,9 @@ def tile_picked_deliver_relu_p_kernel(
             z[t] = keep.tile([P, 2 * S], F32, name="z%d" % t, align_bytes=64)
         got, act = {}, {}
         for t in range(PACK):
-            got[t] = keep.tile([P, V], F32, name="got%d" % t, align_bytes=64)
-            act[t] = keep.tile([P, V], F32, name="act%d" % t, tag="act%d" % t, align_bytes=64)
+            got[t] = keep.tile([P, V], F32, name="got%d" % t, tag="got%d" % t, align_bytes=64)
+        for t, slot in ((1, "act1"), (3, "act3"), (0, "act0"), (2, "act3")):
+            act[t] = keep.tile([P, V], F32, name="act%d" % t, tag=slot, align_bytes=64)
 
         for t in (0, 2):
             nc.vector.memset(z[t][:, S : 2 * S], 0.0)
@@ -149,12 +150,15 @@ def tile_picked_deliver_relu_p_kernel(
                 w2_raw[:, :, mt * P : (mt + 1) * P].rearrange("p j (c i) -> p c j i", i=4),
             )
 
-        def quantize_w2(u, slot):
-            w2_codes[u] = keep.tile([P, HALF], U32, name="w2_codes%d" % u, tag=slot, align_bytes=64)
+        def quantize_w2(mt0, mt1, slot):
+            codes = keep.tile([P, (mt1 - mt0) * P], U32, name="w2_codes%d" % mt0, tag=slot, align_bytes=64)
+            for mt in range(mt0, mt1):
+                w2_codes[mt] = codes[:, (mt - mt0) * P : (mt - mt0 + 1) * P]
+            lo = (mt0 % 2) * P
             nc.vector.quantize_mx(
-                out=w2_codes[u][:].bitcast(FP8X4),
-                scales=w2_scales[:, u * HALF : (u + 1) * HALF],
-                in_=w2_bf[u][:].rearrange("p n j -> p (n j)"),
+                out=codes[:].bitcast(FP8X4),
+                scales=w2_scales[:, mt0 * P : mt1 * P],
+                in_=w2_bf[mt0 // 2][:, lo : lo + (mt1 - mt0) * P, :].rearrange("p n j -> p (n j)"),
             )
 
         chunks = ((0, P), (P, HALF), (HALF, S))
@@ -199,10 +203,11 @@ def tile_picked_deliver_relu_p_kernel(
         join(1)
         deliver(0)
         round_w2(2)
-        activate(2)
         join(3)
+        activate(2)
         round_w2(3)
         deliver(2)
+        quantize_w2(0, 1, "got2")
         for c in range(3):
             nc.scalar.copy(*pair_views(0, c))
 
@@ -210,7 +215,7 @@ def tile_picked_deliver_relu_p_kernel(
             m_cols = slice(mt * P, (mt + 1) * P)
             nc.tensor.matmul_mx(
                 out=dest,
-                lhsT=w2_codes[mt // 2][:, (mt % 2) * P : (mt % 2 + 1) * P].bitcast(FP8X4),
+                lhsT=w2_codes[mt].bitcast(FP8X4),
                 lhsT_scale=w2_scales[:, m_cols],
                 rhs=z_codes[:, j0:j1].bitcast(FP8X4),
                 rhs_scale=z_scales[:, j0:j1],
@@ -234,14 +239,17 @@ def tile_picked_deliver_relu_p_kernel(
         nc.vector.tensor_copy(*pair_views(2, 0))
         nc.scalar.copy(*pair_views(2, 1))
         nc.scalar.copy(*pair_views(2, 2))
-        quantize_w2(0, "act2")
+        quantize_w2(1, 2, "act3")
         quantize_z(0)
         quantize_z(1)
-        quantize_w2(1, "z_bf1")
+        quantize_w2(2, 4, "z_bf1")
         quantize_z(2)
-        output_piece(0, 2, 0, P, False)
+        output_piece(0, 1, 0, P, False)
+        output_piece(1, 2, 0, P, False)
         output_piece(0, 2, P, HALF, False)
         output_piece(2, 3, 0, HALF, True)
         output_piece(3, 4, 0, HALF, False)
-        for mt in range(4):
+        for mt in range(3):
             output_piece(mt, mt + 1, HALF, S, mt % 2 == 0)
+        output_piece(3, 4, HALF, HALF + P, False)
+        output_piece(3, 4, HALF + P, S, True)

@@ -19,6 +19,8 @@ P = 128
 PACK = 4
 HALF = 256
 LIST_COL = 16
+LATE = 96
+FIRST = 768
 
 
 def tile_picked_deliver_relu_p_kernel(
@@ -34,17 +36,21 @@ def tile_picked_deliver_relu_p_kernel(
         dst_t = keep.tile([P, V // LIST_COL], U16, name="dst_t")
         xw = keep.tile([P, T], U32, name="xw", tag="xw", align_bytes=64)
         xs = keep.tile([P, T], U8, name="xs", align_bytes=64)
-        w1_raw = [keep.tile([P, 2, H], F32, name="w1_raw%d" % u, align_bytes=64) for u in range(2)]
+        w1_parts = ((0, 0, P), (1, 0, LATE), (1, LATE, P))
+        w1_raw = [
+            keep.tile([P, 2, PACK * (m1 - m0)], F32, name="w1_raw%d" % i, align_bytes=64)
+            for i, (u, m0, m1) in enumerate(w1_parts)
+        ]
 
         nc.vector.memset(xs[:].bitcast(I32), 0)
         w1_rows = w1.rearrange("(p j) c -> p j c", j=PACK)
         x_cols = x_words[0].rearrange("p n t -> p (n t)").bitcast(I32)
-        nc.sync.dma_start(out=xw[:, 0 : T // 4].bitcast(I32), in_=x_cols[:, 0 : T // 4])
+        nc.sync.dma_start(out=xw[:, 0 : FIRST].bitcast(I32), in_=x_cols[:, 0 : FIRST])
         nc.sync.dma_start(offs_t[:], offs)
         nc.sync.dma_start(out=xs[0:P:8, :].bitcast(I32), in_=x_scales[0].bitcast(I32))
-        nc.sync.dma_start(out=xw[:, T // 4 : T].bitcast(I32), in_=x_cols[:, T // 4 : T])
-        nc.sync.dma_start(out=w1_raw[0][:], in_=w1_rows[:, 0:2, :])
-        nc.sync.dma_start(out=w1_raw[1][:], in_=w1_rows[:, 2:PACK, :])
+        nc.sync.dma_start(out=xw[:, FIRST : T].bitcast(I32), in_=x_cols[:, FIRST : T])
+        for i, (u, m0, m1) in enumerate(w1_parts):
+            nc.sync.dma_start(out=w1_raw[i][:], in_=w1_rows[:, 2 * u : 2 * u + 2, PACK * m0 : PACK * m1])
         nc.sync.dma_start(src_t[:], src)
         nc.sync.dma_start(dst_t[:], dst)
 
@@ -56,9 +62,10 @@ def tile_picked_deliver_relu_p_kernel(
             w1_codes[e] = keep.tile([P, 2 * P], U32, name="w1_codes%d" % e, align_bytes=64)
             w1_scales[e] = keep.tile([P, 2 * P], U8, name="w1_scales%d" % e, align_bytes=64)
 
-        def w1_views(e, u):
-            cols = w1_raw[u][:].rearrange("p j (m s e) -> p e m j s", s=2, e=2)
-            return w1_bf[e][:, :, :, 2 * u : 2 * u + 2].rearrange("p s m j -> p m j s"), cols[:, e]
+        def w1_views(e, i):
+            u, m0, m1 = w1_parts[i]
+            cols = w1_raw[i][:].rearrange("p j (m s e) -> p e m j s", s=2, e=2)
+            return w1_bf[e][:, :, m0:m1, 2 * u : 2 * u + 2].rearrange("p s m j -> p m j s"), cols[:, e]
 
         def quantize_w1(e, s0, s1):
             nc.vector.quantize_mx(
@@ -78,10 +85,9 @@ def tile_picked_deliver_relu_p_kernel(
         nc.sync.dma_start(out=w2_raw[:], in_=w2.rearrange("(p j) c -> p j c", j=PACK))
         nc.vector.tensor_copy(*w1_views(1, 0))
         nc.scalar.activation(*w1_views(0, 0), COPY)
-        late_out, late_in = w1_views(1, 1)
-        for s in range(2):
-            nc.vector.tensor_copy(late_out[:, :, :, s], late_in[:, :, :, s])
-        nc.scalar.activation(*w1_views(0, 1), COPY)
+        for i in (1, 2):
+            nc.vector.tensor_copy(*w1_views(1, i))
+            nc.scalar.activation(*w1_views(0, i), COPY)
         quantize_w1(1, 0, 1)
         quantize_w1(1, 1, 2)
         quantize_w1(0, 0, 2)

@@ -49,12 +49,21 @@ def tile_picked_deliver_relu_p_kernel(
         nc.sync.dma_start(offs_t[:], offs)
         nc.sync.dma_start(out=xs[0:P:8, :].bitcast(I32), in_=x_scales[0].bitcast(I32))
         nc.sync.dma_start(out=xw[:, FIRST : T].bitcast(I32), in_=x_cols[:, FIRST : T])
+        nc.sync.dma_start(src_t[:], src)
         for i, (u, m0, m1) in enumerate(w1_parts):
             nc.sync.dma_start(out=w1_raw[i][:], in_=w1_rows[:, 2 * u : 2 * u + 2, PACK * m0 : PACK * m1])
-        nc.sync.dma_start(src_t[:], src)
         nc.sync.dma_start(dst_t[:], dst)
 
+        z = {}
+        for t in (1, 3):
+            z[t] = keep.tile([P, S], F32, name="z%d" % t, align_bytes=64)
+        for t in (0, 2):
+            z[t] = keep.tile([P, 2 * S], F32, name="z%d" % t, align_bytes=64)
+        nc.vector.memset(z[0][:, S : 2 * S], 0.0)
+        nc.scalar.activation(z[2][:, S : 2 * S], z[0][:, S : 2 * S], COPY)
+
         xs_g = keep.tile([P, S], U8, name="xs_g", align_bytes=64)
+        nc.vector.memset(xs_g[:].bitcast(I32), 0)
 
         w1_codes, w1_scales, w1_bf = {}, {}, {}
         for e in (1, 0):
@@ -77,9 +86,8 @@ def tile_picked_deliver_relu_p_kernel(
         xw_g = keep.tile([P, S], U32, name="xw_g", align_bytes=64)
         xs_spread = keep.tile([P, S], U8, name="xs_spread", align_bytes=64)
         nc.vector.tensor_copy(out=xs_spread[:], in_=xs[:].indirect(offs_t[:]))
-        nc.vector.tensor_copy(out=xs_g[:].bitcast(I32), in_=xs_spread[:].bitcast(I32))
-        for r in range(1, 4):
-            nc.sync.dma_start(out=xs_g[r:P:32, :].bitcast(I32), in_=xs_spread[8 * r : P : 32, :].bitcast(I32))
+        for r in range(4):
+            nc.scalar.dma_start(out=xs_g[r:P:32, :].bitcast(I32), in_=xs_spread[8 * r : P : 32, :].bitcast(I32))
         nc.vector.tensor_copy(out=xw_g[:], in_=xw[:].indirect(offs_t[:]))
         w2_raw = keep.tile([P, PACK, N], F32, name="w2_raw", tag="xw", align_bytes=64)
         nc.sync.dma_start(out=w2_raw[:], in_=w2.rearrange("(p j) c -> p j c", j=PACK))
@@ -106,19 +114,12 @@ def tile_picked_deliver_relu_p_kernel(
             )
             return bank
 
-        z = {}
-        for t in (1, 3):
-            z[t] = keep.tile([P, S], F32, name="z%d" % t, align_bytes=64)
-        for t in (0, 2):
-            z[t] = keep.tile([P, 2 * S], F32, name="z%d" % t, align_bytes=64)
         got, act = {}, {}
         for t in range(PACK):
             got[t] = keep.tile([P, V], F32, name="got%d" % t, tag="got%d" % t, align_bytes=64)
         for t, slot in ((1, "act1"), (3, "act3"), (0, "act0"), (2, "act3")):
             act[t] = keep.tile([P, V], F32, name="act%d" % t, tag=slot, align_bytes=64)
 
-        for t in (0, 2):
-            nc.vector.memset(z[t][:, S : 2 * S], 0.0)
 
         warm = psum.tile([P, S], F32, name="warm", tag="bank")
         for u in range(2):

@@ -19,7 +19,6 @@ P = 128
 PACK = 4
 HALF = 256
 LIST_COL = 16
-LATE = 96
 FIRST = 768
 
 
@@ -35,8 +34,8 @@ def tile_picked_deliver_relu_p_kernel(
         src_t = keep.tile([P, V // LIST_COL], U16, name="src_t")
         dst_t = keep.tile([P, V // LIST_COL], U16, name="dst_t")
         xw = keep.tile([P, T], U32, name="xw", tag="xw", align_bytes=64)
-        xs = keep.tile([P, T], U8, name="xs", align_bytes=64)
-        w1_parts = ((0, 0, P), (1, 0, LATE), (1, LATE, P))
+        xs = keep.tile([P, T], U8, name="xs", tag="xs", align_bytes=64)
+        w1_parts = ((0, 0, P), (1, 0, P))
         w1_raw = [
             keep.tile([P, 2, PACK * (m1 - m0)], F32, name="w1_raw%d" % i, align_bytes=64)
             for i, (u, m0, m1) in enumerate(w1_parts)
@@ -49,10 +48,8 @@ def tile_picked_deliver_relu_p_kernel(
         nc.sync.dma_start(offs_t[:], offs)
         nc.sync.dma_start(out=xs[0:P:8, :].bitcast(I32), in_=x_scales[0].bitcast(I32))
         nc.sync.dma_start(out=xw[:, FIRST : T].bitcast(I32), in_=x_cols[:, FIRST : T])
-        nc.sync.dma_start(src_t[:], src)
         for i, (u, m0, m1) in enumerate(w1_parts):
             nc.sync.dma_start(out=w1_raw[i][:], in_=w1_rows[:, 2 * u : 2 * u + 2, PACK * m0 : PACK * m1])
-        nc.sync.dma_start(dst_t[:], dst)
 
         z = {}
         for t in (1, 3):
@@ -87,15 +84,22 @@ def tile_picked_deliver_relu_p_kernel(
         xs_spread = keep.tile([P, S], U8, name="xs_spread", align_bytes=64)
         nc.vector.tensor_copy(out=xs_spread[:], in_=xs[:].indirect(offs_t[:]))
         for r in range(4):
-            nc.scalar.dma_start(out=xs_g[r:P:32, :].bitcast(I32), in_=xs_spread[8 * r : P : 32, :].bitcast(I32))
+            nc.sync.dma_start(out=xs_g[r:P:32, :].bitcast(I32), in_=xs_spread[8 * r : P : 32, :].bitcast(I32))
+        nc.sync.dma_start(src_t[:], src)
+        nc.sync.dma_start(dst_t[:], dst)
         nc.vector.tensor_copy(out=xw_g[:], in_=xw[:].indirect(offs_t[:]))
-        w2_raw = keep.tile([P, PACK, N], F32, name="w2_raw", tag="xw", align_bytes=64)
-        nc.sync.dma_start(out=w2_raw[:], in_=w2.rearrange("(p j) c -> p j c", j=PACK))
+        w2_raw = []
+        for u, slot in enumerate(("xs", "xw")):
+            w2_raw.append(keep.tile([P, PACK, HALF], F32, name="w2_raw%d" % u, tag=slot, align_bytes=64))
+            nc.sync.dma_start(
+                out=w2_raw[u][:], in_=w2.rearrange("(p j) c -> p j c", j=PACK)[:, :, u * HALF : (u + 1) * HALF]
+            )
         nc.vector.tensor_copy(*w1_views(1, 0))
         nc.scalar.activation(*w1_views(0, 0), COPY)
-        for i in (1, 2):
-            nc.vector.tensor_copy(*w1_views(1, i))
-            nc.scalar.activation(*w1_views(0, i), COPY)
+        late_out, late_in = w1_views(1, 1)
+        for s in range(2):
+            nc.vector.tensor_copy(late_out[:, :, :, s], late_in[:, :, :, s])
+        nc.scalar.activation(*w1_views(0, 1), COPY)
         quantize_w1(1, 0, 1)
         quantize_w1(1, 1, 2)
         quantize_w1(0, 0, 2)
@@ -116,8 +120,8 @@ def tile_picked_deliver_relu_p_kernel(
 
         got, act = {}, {}
         for t in range(PACK):
-            got[t] = keep.tile([P, V], F32, name="got%d" % t, tag="got%d" % t, align_bytes=64)
-        for t, slot in ((1, "act1"), (3, "act3"), (0, "act0"), (2, "act3")):
+            got[t] = keep.tile([P, V], F32, name="got%d" % t, tag="got%d" % (t if t % 2 else 2), align_bytes=64)
+        for t, slot in ((1, "act1"), (3, "act3"), (0, "xs"), (2, "act3")):
             act[t] = keep.tile([P, V], F32, name="act%d" % t, tag=slot, align_bytes=64)
 
 
@@ -154,7 +158,7 @@ def tile_picked_deliver_relu_p_kernel(
             lo = (mt % 2) * P
             nc.scalar.copy(
                 w2_bf[mt // 2][:, lo : lo + P, :].rearrange("p (c i) j -> p c j i", i=4),
-                w2_raw[:, :, mt * P : (mt + 1) * P].rearrange("p j (c i) -> p c j i", i=4),
+                w2_raw[mt // 2][:, :, lo : lo + P].rearrange("p j (c i) -> p c j i", i=4),
             )
 
         def quantize_w2(mt0, mt1, slot):
@@ -232,16 +236,25 @@ def tile_picked_deliver_relu_p_kernel(
 
         out_rows = out.rearrange("(mt p) j -> p mt j", p=P)
 
-        def output_piece(mt0, mt1, j0, j1, on_vector):
+        def product_part(res, mt0, mt1, j0, j1, on_vector):
             bank = psum.tile([P, mt1 - mt0, j1 - j0], F32, name="bank", tag="bank")
             for mt in range(mt0, mt1):
                 second_product(mt, j0, j1, bank[:, mt - mt0, :])
-            res = keep.tile([P, mt1 - mt0, j1 - j0], F32, name="res%d_%d" % (mt0, j0), align_bytes=64)
             if on_vector:
-                nc.vector.tensor_copy(out=res[:], in_=bank[:])
+                nc.vector.tensor_copy(out=res, in_=bank[:])
             else:
-                nc.scalar.copy(res[:], bank[:])
+                nc.scalar.copy(res, bank[:])
+
+        def result_tile(mt0, mt1, j0, j1):
+            return keep.tile([P, mt1 - mt0, j1 - j0], F32, name="res%d_%d" % (mt0, j0), align_bytes=64)
+
+        def store(res, mt0, mt1, j0, j1):
             nc.sync.dma_start(out=out_rows[:, mt0:mt1, j0:j1], in_=res[:])
+
+        def output_piece(mt0, mt1, j0, j1, on_vector):
+            res = result_tile(mt0, mt1, j0, j1)
+            product_part(res[:], mt0, mt1, j0, j1, on_vector)
+            store(res, mt0, mt1, j0, j1)
 
         nc.vector.tensor_copy(*pair_views(2, 0))
         nc.scalar.copy(*pair_views(2, 1))
@@ -258,5 +271,7 @@ def tile_picked_deliver_relu_p_kernel(
         output_piece(3, 4, 0, HALF, False)
         for mt in range(3):
             output_piece(mt, mt + 1, HALF, S, mt % 2 == 0)
-        output_piece(3, 4, HALF, HALF + P, False)
-        output_piece(3, 4, HALF + P, S, True)
+        last = result_tile(3, 4, HALF, S)
+        product_part(last[:, :, 0:P], 3, 4, HALF, HALF + P, False)
+        product_part(last[:, :, P:HALF], 3, 4, HALF + P, S, True)
+        store(last, 3, 4, HALF, S)

@@ -19,7 +19,8 @@ P = 128
 PACK = 4
 HALF = 256
 LIST_COL = 16
-FIRST = 768
+FIRST = 1024
+LATE = 96
 
 
 def tile_picked_deliver_relu_p_kernel(
@@ -35,7 +36,7 @@ def tile_picked_deliver_relu_p_kernel(
         dst_t = keep.tile([P, V // LIST_COL], U16, name="dst_t")
         xw = keep.tile([P, T], U32, name="xw", tag="xw", align_bytes=64)
         xs = keep.tile([P, T], U8, name="xs", tag="xs", align_bytes=64)
-        w1_parts = ((0, 0, P), (1, 0, P))
+        w1_parts = ((0, 0, P), (1, 0, LATE), (1, LATE, P))
         w1_raw = [
             keep.tile([P, 2, PACK * (m1 - m0)], F32, name="w1_raw%d" % i, align_bytes=64)
             for i, (u, m0, m1) in enumerate(w1_parts)
@@ -96,10 +97,9 @@ def tile_picked_deliver_relu_p_kernel(
             )
         nc.vector.tensor_copy(*w1_views(1, 0))
         nc.scalar.activation(*w1_views(0, 0), COPY)
-        late_out, late_in = w1_views(1, 1)
-        for s in range(2):
-            nc.vector.tensor_copy(late_out[:, :, :, s], late_in[:, :, :, s])
-        nc.scalar.activation(*w1_views(0, 1), COPY)
+        for i in (1, 2):
+            nc.vector.tensor_copy(*w1_views(1, i))
+            nc.scalar.activation(*w1_views(0, i), COPY)
         quantize_w1(1, 0, 1)
         quantize_w1(1, 1, 2)
         quantize_w1(0, 0, 2)
@@ -150,48 +150,48 @@ def tile_picked_deliver_relu_p_kernel(
         def join(t):
             nc.scalar.copy(z[t - 1][:, S : 2 * S], z[t][:])
 
-        w2_bf = [keep.tile([P, HALF, PACK], BF16, name="w2_bf%d" % u, align_bytes=64) for u in range(2)]
-        w2_scales = keep.tile([P, N], U8, name="w2_scales", align_bytes=64)
-        w2_codes = {}
+        late_bf = keep.tile([P, 6 * P, PACK], BF16, name="late_bf", align_bytes=64)
+        late_codes = keep.tile([P, 6 * P], U32, name="late_codes", align_bytes=64)
+        late_scales = keep.tile([P, 6 * P], U8, name="late_scales", align_bytes=64)
+        early_bf = keep.tile([P, HALF, PACK], BF16, name="early_bf", align_bytes=64)
+        early_scales = keep.tile([P, HALF], U8, name="early_scales", align_bytes=64)
+        w2_codes, w2_scales = {}, {}
+        for mt in (2, 3):
+            w2_codes[mt] = late_codes[:, mt * P : (mt + 1) * P]
+            w2_scales[mt] = late_scales[:, mt * P : (mt + 1) * P]
+
+        def token_cols(j0, j1):
+            shift = 0 if j0 < HALF else HALF
+            return slice(j0 + shift, j1 + shift)
 
         def round_w2(mt):
             lo = (mt % 2) * P
+            dest = early_bf if mt < 2 else late_bf
             nc.scalar.copy(
-                w2_bf[mt // 2][:, lo : lo + P, :].rearrange("p (c i) j -> p c j i", i=4),
+                dest[:, mt * P : (mt + 1) * P, :].rearrange("p (c i) j -> p c j i", i=4),
                 w2_raw[mt // 2][:, :, lo : lo + P].rearrange("p j (c i) -> p c j i", i=4),
             )
 
-        def quantize_w2(mt0, mt1, slot):
-            codes = keep.tile([P, (mt1 - mt0) * P], U32, name="w2_codes%d" % mt0, tag=slot, align_bytes=64)
-            for mt in range(mt0, mt1):
-                w2_codes[mt] = codes[:, (mt - mt0) * P : (mt - mt0 + 1) * P]
-            lo = (mt0 % 2) * P
+        def quantize_w2(mt, slot):
+            codes = keep.tile([P, P], U32, name="w2_codes%d" % mt, tag=slot, align_bytes=64)
+            w2_codes[mt] = codes[:]
+            w2_scales[mt] = early_scales[:, mt * P : (mt + 1) * P]
             nc.vector.quantize_mx(
                 out=codes[:].bitcast(FP8X4),
-                scales=w2_scales[:, mt0 * P : mt1 * P],
-                in_=w2_bf[mt0 // 2][:, lo : lo + (mt1 - mt0) * P, :].rearrange("p n j -> p (n j)"),
+                scales=w2_scales[mt],
+                in_=early_bf[:, mt * P : (mt + 1) * P, :].rearrange("p n j -> p (n j)"),
             )
 
-        chunks = ((0, P), (P, HALF), (HALF, S))
-        z_bf = [
-            keep.tile([P, j1 - j0, PACK], BF16, name="z_bf%d" % c, tag="z_bf%d" % c, align_bytes=64)
-            for c, (j0, j1) in enumerate(chunks)
-        ]
-        z_codes = keep.tile([P, S], U32, name="z_codes", align_bytes=64)
-        z_scales = keep.tile([P, S], U8, name="z_scales", align_bytes=64)
-
-        def quantize_z(c):
-            j0, j1 = chunks[c]
+        def quantize_late(b0, b1):
             nc.vector.quantize_mx(
-                out=z_codes[:, j0:j1].bitcast(FP8X4),
-                scales=z_scales[:, j0:j1],
-                in_=z_bf[c][:].rearrange("p n j -> p (n j)"),
+                out=late_codes[:, b0 * P : b1 * P].bitcast(FP8X4),
+                scales=late_scales[:, b0 * P : b1 * P],
+                in_=late_bf[:, b0 * P : b1 * P, :].rearrange("p n j -> p (n j)"),
             )
 
-        def pair_views(t, c):
-            j0, j1 = chunks[c]
+        def pair_views(t, j0, j1):
             pair = z[t][:].rearrange("p (s n) -> p n s", s=2)
-            return z_bf[c][:, :, t : t + 2], pair[:, j0:j1, :]
+            return late_bf[:, token_cols(j0, j1), t : t + 2], pair[:, j0:j1, :]
 
         for t, q, bank in early:
             if (t, q) in ((1, 1), (1, 3), (3, 0)):
@@ -218,18 +218,17 @@ def tile_picked_deliver_relu_p_kernel(
         activate(2)
         round_w2(3)
         deliver(2)
-        quantize_w2(0, 1, "got2")
-        for c in range(3):
-            nc.scalar.copy(*pair_views(0, c))
+        quantize_w2(0, "got2")
+        for j0, j1 in ((0, P), (P, HALF), (HALF, S)):
+            nc.scalar.copy(*pair_views(0, j0, j1))
 
         def second_product(mt, j0, j1, dest):
-            m_cols = slice(mt * P, (mt + 1) * P)
             nc.tensor.matmul_mx(
                 out=dest,
                 lhsT=w2_codes[mt].bitcast(FP8X4),
-                lhsT_scale=w2_scales[:, m_cols],
-                rhs=z_codes[:, j0:j1].bitcast(FP8X4),
-                rhs_scale=z_scales[:, j0:j1],
+                lhsT_scale=w2_scales[mt],
+                rhs=late_codes[:, token_cols(j0, j1)].bitcast(FP8X4),
+                rhs_scale=late_scales[:, token_cols(j0, j1)],
                 start=True,
                 stop=True,
             )
@@ -256,14 +255,14 @@ def tile_picked_deliver_relu_p_kernel(
             product_part(res[:], mt0, mt1, j0, j1, on_vector)
             store(res, mt0, mt1, j0, j1)
 
-        nc.vector.tensor_copy(*pair_views(2, 0))
-        nc.scalar.copy(*pair_views(2, 1))
-        nc.scalar.copy(*pair_views(2, 2))
-        quantize_w2(1, 2, "act3")
-        quantize_z(0)
-        quantize_z(1)
-        quantize_w2(2, 4, "z_bf1")
-        quantize_z(2)
+        nc.vector.tensor_copy(*pair_views(2, 0, P))
+        for b in range(1, 4):
+            nc.scalar.copy(*pair_views(2, b * P, (b + 1) * P))
+        quantize_w2(1, "act3")
+        quantize_late(0, 1)
+        quantize_late(1, 3)
+        quantize_late(3, 5)
+        quantize_late(5, 6)
         output_piece(0, 1, 0, P, False)
         output_piece(1, 2, 0, P, False)
         output_piece(0, 2, P, HALF, False)

@@ -19,8 +19,11 @@ P = 128
 PACK = 4
 HALF = 256
 LIST_COL = 16
-FIRST = 1024
-LATE = 96
+QUADRANT = 32
+SPREAD = 8
+BANKS = 8
+X_FIRST = 896
+W1_LAST = 96
 
 
 def tile_picked_deliver_relu_p_kernel(
@@ -29,14 +32,14 @@ def tile_picked_deliver_relu_p_kernel(
     nc = tc.nc
     with ExitStack() as ctx:
         keep = ctx.enter_context(tc.tile_pool(name="keep", bufs=1))
-        psum = ctx.enter_context(tc.psum_pool(name="psum", bufs=8))
+        psum = ctx.enter_context(tc.psum_pool(name="psum", bufs=BANKS))
 
         offs_t = keep.tile([P, S // LIST_COL], U16, name="offs_t")
         src_t = keep.tile([P, V // LIST_COL], U16, name="src_t")
         dst_t = keep.tile([P, V // LIST_COL], U16, name="dst_t")
-        xw = keep.tile([P, T], U32, name="xw", tag="xw", align_bytes=64)
-        xs = keep.tile([P, T], U8, name="xs", tag="xs", align_bytes=64)
-        w1_parts = ((0, 0, P), (1, 0, LATE), (1, LATE, P))
+        xw = keep.tile([P, T], U32, name="xw", tag="slot_xw", align_bytes=64)
+        xs = keep.tile([P, T], U8, name="xs", tag="slot_xs", align_bytes=64)
+        w1_parts = ((0, 0, P), (1, 0, W1_LAST), (1, W1_LAST, P))
         w1_raw = [
             keep.tile([P, 2, PACK * (m1 - m0)], F32, name="w1_raw%d" % i, align_bytes=64)
             for i, (u, m0, m1) in enumerate(w1_parts)
@@ -45,10 +48,10 @@ def tile_picked_deliver_relu_p_kernel(
         nc.vector.memset(xs[:].bitcast(I32), 0)
         w1_rows = w1.rearrange("(p j) c -> p j c", j=PACK)
         x_cols = x_words[0].rearrange("p n t -> p (n t)").bitcast(I32)
-        nc.sync.dma_start(out=xw[:, 0 : FIRST].bitcast(I32), in_=x_cols[:, 0 : FIRST])
+        nc.sync.dma_start(out=xw[:, 0:X_FIRST].bitcast(I32), in_=x_cols[:, 0:X_FIRST])
         nc.sync.dma_start(offs_t[:], offs)
-        nc.sync.dma_start(out=xs[0:P:8, :].bitcast(I32), in_=x_scales[0].bitcast(I32))
-        nc.sync.dma_start(out=xw[:, FIRST : T].bitcast(I32), in_=x_cols[:, FIRST : T])
+        nc.sync.dma_start(out=xs[0:P:SPREAD, :].bitcast(I32), in_=x_scales[0].bitcast(I32))
+        nc.sync.dma_start(out=xw[:, X_FIRST:T].bitcast(I32), in_=x_cols[:, X_FIRST:T])
         for i, (u, m0, m1) in enumerate(w1_parts):
             nc.sync.dma_start(out=w1_raw[i][:], in_=w1_rows[:, 2 * u : 2 * u + 2, PACK * m0 : PACK * m1])
 
@@ -84,49 +87,54 @@ def tile_picked_deliver_relu_p_kernel(
         xw_g = keep.tile([P, S], U32, name="xw_g", align_bytes=64)
         xs_spread = keep.tile([P, S], U8, name="xs_spread", align_bytes=64)
         nc.vector.tensor_copy(out=xs_spread[:], in_=xs[:].indirect(offs_t[:]))
-        for r in range(4):
-            nc.sync.dma_start(out=xs_g[r:P:32, :].bitcast(I32), in_=xs_spread[8 * r : P : 32, :].bitcast(I32))
+        for r in range(QUADRANT // SPREAD):
+            nc.sync.dma_start(
+                out=xs_g[r:P:QUADRANT, :].bitcast(I32), in_=xs_spread[SPREAD * r : P : QUADRANT, :].bitcast(I32)
+            )
         nc.sync.dma_start(src_t[:], src)
         nc.sync.dma_start(dst_t[:], dst)
         nc.vector.tensor_copy(out=xw_g[:], in_=xw[:].indirect(offs_t[:]))
         w2_raw = []
-        for u, slot in enumerate(("xs", "xw")):
+        for u, slot in enumerate(("slot_xs", "slot_xw")):
             w2_raw.append(keep.tile([P, PACK, HALF], F32, name="w2_raw%d" % u, tag=slot, align_bytes=64))
             nc.sync.dma_start(
                 out=w2_raw[u][:], in_=w2.rearrange("(p j) c -> p j c", j=PACK)[:, :, u * HALF : (u + 1) * HALF]
             )
+
         nc.vector.tensor_copy(*w1_views(1, 0))
         nc.scalar.activation(*w1_views(0, 0), COPY)
+        nc.vector.tensor_copy(*w1_views(1, 1))
+        last_out, last_in = w1_views(1, 2)
+        for s in range(2):
+            nc.vector.tensor_copy(last_out[:, :, :, s], last_in[:, :, :, s])
         for i in (1, 2):
-            nc.vector.tensor_copy(*w1_views(1, i))
             nc.scalar.activation(*w1_views(0, i), COPY)
         quantize_w1(1, 0, 1)
         quantize_w1(1, 1, 2)
         quantize_w1(0, 0, 2)
 
-        def first_product(t, c0, c1):
-            bank = psum.tile([P, c1 - c0], F32, name="bank", tag="bank")
+        def first_product(t, j0, j1):
+            bank = psum.tile([P, j1 - j0], F32, name="bank", tag="bank")
             m_cols = slice((t // 2) * P, (t // 2 + 1) * P)
             nc.tensor.matmul_mx(
                 out=bank[:],
                 lhsT=w1_codes[t % 2][:, m_cols].bitcast(FP8X4),
                 lhsT_scale=w1_scales[t % 2][:, m_cols],
-                rhs=xw_g[:, c0:c1].bitcast(FP8X4),
-                rhs_scale=xs_g[:, c0:c1],
+                rhs=xw_g[:, j0:j1].bitcast(FP8X4),
+                rhs_scale=xs_g[:, j0:j1],
                 start=True,
                 stop=True,
             )
             return bank
 
         got, act = {}, {}
-        for t in range(PACK):
-            got[t] = keep.tile([P, V], F32, name="got%d" % t, tag="got%d" % (t if t % 2 else 2), align_bytes=64)
-        for t, slot in ((1, "act1"), (3, "act3"), (0, "xs"), (2, "act3")):
+        for t, slot in enumerate(("slot_even", "got1", "slot_even", "got3")):
+            got[t] = keep.tile([P, V], F32, name="got%d" % t, tag=slot, align_bytes=64)
+        for t, slot in ((1, "act1"), (3, "slot_act"), (0, "slot_xs"), (2, "slot_act")):
             act[t] = keep.tile([P, V], F32, name="act%d" % t, tag=slot, align_bytes=64)
 
-
         warm = psum.tile([P, S], F32, name="warm", tag="bank")
-        for u in range(2):
+        for warm_pass in range(2):
             nc.tensor.matmul_mx(
                 out=warm[:],
                 lhsT=xw_g[:, 0:P].bitcast(FP8X4),
@@ -136,7 +144,7 @@ def tile_picked_deliver_relu_p_kernel(
                 start=True,
                 stop=True,
             )
-        early = [(t, q, first_product(t, q * P, (q + 1) * P)) for t in (1, 3) for q in range(4)]
+        odd_blocks = [(t, b, first_product(t, b * P, (b + 1) * P)) for t in (1, 3) for b in range(S // P)]
 
         def fetch(t):
             nc.vector.tensor_copy(out=got[t][:], in_=z[t][:].indirect(src_t[:]))
@@ -172,7 +180,7 @@ def tile_picked_deliver_relu_p_kernel(
                 w2_raw[mt // 2][:, :, lo : lo + P].rearrange("p j (c i) -> p c j i", i=4),
             )
 
-        def quantize_w2(mt, slot):
+        def quantize_early(mt, slot):
             codes = keep.tile([P, P], U32, name="w2_codes%d" % mt, tag=slot, align_bytes=64)
             w2_codes[mt] = codes[:]
             w2_scales[mt] = early_scales[:, mt * P : (mt + 1) * P]
@@ -193,11 +201,11 @@ def tile_picked_deliver_relu_p_kernel(
             pair = z[t][:].rearrange("p (s n) -> p n s", s=2)
             return late_bf[:, token_cols(j0, j1), t : t + 2], pair[:, j0:j1, :]
 
-        for t, q, bank in early:
-            if (t, q) in ((1, 1), (1, 3), (3, 0)):
-                nc.vector.tensor_copy(z[t][:, q * P : (q + 1) * P], bank[:])
+        for t, b, bank in odd_blocks:
+            if (b % 2 == 1) if t == 1 else (b == 0):
+                nc.vector.tensor_copy(z[t][:, b * P : (b + 1) * P], bank[:])
             else:
-                nc.scalar.copy(z[t][:, q * P : (q + 1) * P], bank[:])
+                nc.scalar.copy(z[t][:, b * P : (b + 1) * P], bank[:])
         fetch(1)
         fetch(3)
         activate(1)
@@ -218,7 +226,7 @@ def tile_picked_deliver_relu_p_kernel(
         activate(2)
         round_w2(3)
         deliver(2)
-        quantize_w2(0, "got2")
+        quantize_early(0, "slot_even")
         for j0, j1 in ((0, P), (P, HALF), (HALF, S)):
             nc.scalar.copy(*pair_views(0, j0, j1))
 
@@ -256,13 +264,11 @@ def tile_picked_deliver_relu_p_kernel(
             store(res, mt0, mt1, j0, j1)
 
         nc.vector.tensor_copy(*pair_views(2, 0, P))
-        for b in range(1, 4):
+        for b in range(1, S // P):
             nc.scalar.copy(*pair_views(2, b * P, (b + 1) * P))
-        quantize_w2(1, "act3")
-        quantize_late(0, 1)
-        quantize_late(1, 3)
-        quantize_late(3, 5)
-        quantize_late(5, 6)
+        quantize_early(1, "slot_act")
+        for b0, b1 in ((0, 1), (1, 3), (3, 5), (5, 6)):
+            quantize_late(b0, b1)
         output_piece(0, 1, 0, P, False)
         output_piece(1, 2, 0, P, False)
         output_piece(0, 2, P, HALF, False)

@@ -133,17 +133,6 @@ def tile_picked_deliver_relu_p_kernel(
         for t, slot in ((1, "act1"), (3, "slot_act"), (0, "slot_xs"), (2, "slot_act")):
             act[t] = keep.tile([P, V], F32, name="act%d" % t, tag=slot, align_bytes=64)
 
-        warm = psum.tile([P, S], F32, name="warm", tag="bank")
-        for warm_pass in range(2):
-            nc.tensor.matmul_mx(
-                out=warm[:],
-                lhsT=xw_g[:, 0:P].bitcast(FP8X4),
-                lhsT_scale=xs_spread[:, 0:P],
-                rhs=xw_g[:].bitcast(FP8X4),
-                rhs_scale=xs_spread[:],
-                start=True,
-                stop=True,
-            )
         odd_blocks = [(t, b, first_product(t, b * P, (b + 1) * P)) for t in (1, 3) for b in range(S // P)]
 
         def fetch(t):

@@ -14,6 +14,8 @@ U8 = mybir.dt.uint8
 FP8X4 = mybir.dt.float8_e4m3fn_x4
 COPY = mybir.ActivationFunctionType.Copy
 RELU = mybir.ActivationFunctionType.Relu
+MULT = mybir.AluOpType.mult
+ADD = mybir.AluOpType.add
 
 P = 128
 PACK = 4
@@ -57,9 +59,9 @@ def tile_picked_deliver_relu_p_kernel(
 
         z = {}
         for t in (1, 3):
-            z[t] = keep.tile([P, S], F32, name="z%d" % t, align_bytes=64)
+            z[t] = keep.tile([P, S], F32, name="z%d" % t, tag="slot_z%d" % t, align_bytes=64)
         for t in (0, 2):
-            z[t] = keep.tile([P, 2 * S], F32, name="z%d" % t, align_bytes=64)
+            z[t] = keep.tile([P, 2 * S], F32, name="z%d" % t, tag="slot_z%d" % t, align_bytes=64)
         nc.vector.memset(z[0][:, S : 2 * S], 0.0)
         nc.scalar.activation(z[2][:, S : 2 * S], z[0][:, S : 2 * S], COPY)
 
@@ -68,7 +70,7 @@ def tile_picked_deliver_relu_p_kernel(
 
         w1_codes, w1_scales, w1_bf = {}, {}, {}
         for e in (1, 0):
-            w1_bf[e] = keep.tile([P, 2, P, PACK], BF16, name="w1_bf%d" % e, align_bytes=64)
+            w1_bf[e] = keep.tile([P, 2, P, PACK], BF16, name="w1_bf%d" % e, tag="slot_w1bf%d" % e, align_bytes=64)
             w1_codes[e] = keep.tile([P, 2 * P], U32, name="w1_codes%d" % e, align_bytes=64)
             w1_scales[e] = keep.tile([P, 2 * P], U8, name="w1_scales%d" % e, align_bytes=64)
 
@@ -128,15 +130,15 @@ def tile_picked_deliver_relu_p_kernel(
             return bank
 
         got, act = {}, {}
-        for t, slot in enumerate(("slot_even", "got1", "slot_even", "got3")):
+        for t, slot in ((3, "got3"), (0, "slot_even"), (2, "slot_even")):
             got[t] = keep.tile([P, V], F32, name="got%d" % t, tag=slot, align_bytes=64)
-        for t, slot in ((1, "act1"), (3, "slot_act"), (0, "slot_xs"), (2, "slot_act")):
+        for t, slot in ((1, "act1"), (3, "slot_act"), (0, "act0"), (2, "slot_act")):
             act[t] = keep.tile([P, V], F32, name="act%d" % t, tag=slot, align_bytes=64)
 
-        odd_blocks = [(t, b, first_product(t, b * P, (b + 1) * P)) for t in (1, 3) for b in range(S // P)]
+        relu1 = keep.tile([P, S], F32, name="relu1", align_bytes=64)
 
         def fetch(t):
-            nc.vector.tensor_copy(out=got[t][:], in_=z[t][:].indirect(src_t[:]))
+            nc.scalar.activation(got[t][:], z[t][:].indirect(src_t[:]), COPY)
 
         def activate(t):
             nc.scalar.activation(act[t][:], got[t][:], RELU)
@@ -145,77 +147,82 @@ def tile_picked_deliver_relu_p_kernel(
             nc.vector.tensor_copy(out=z[t][:].indirect(dst_t[:]), in_=act[t][:])
 
         def join(t):
-            nc.scalar.copy(z[t - 1][:, S : 2 * S], z[t][:])
+            nc.gpsimd.tensor_scalar(z[t - 1][:, S : 2 * S], z[t][:], 1.0, 0.0, MULT, ADD)
 
-        late_bf = keep.tile([P, 6 * P, PACK], BF16, name="late_bf", align_bytes=64)
-        late_codes = keep.tile([P, 6 * P], U32, name="late_codes", align_bytes=64)
-        late_scales = keep.tile([P, 6 * P], U8, name="late_scales", align_bytes=64)
-        early_bf = keep.tile([P, HALF, PACK], BF16, name="early_bf", align_bytes=64)
-        early_scales = keep.tile([P, HALF], U8, name="early_scales", align_bytes=64)
+        w2_bf = keep.tile([P, N, PACK], BF16, name="w2_bf", tag="slot_w1bf0", align_bytes=64)
+        w2_scale_bytes = keep.tile([P, N], U8, name="w2_scale_bytes", align_bytes=64)
+        z_bf = keep.tile([P, S, PACK], BF16, name="z_bf", tag="slot_even", align_bytes=64)
+        z_codes = keep.tile([P, S], U32, name="z_codes", align_bytes=64)
+        z_scales = keep.tile([P, S], U8, name="z_scales", align_bytes=64)
         w2_codes, w2_scales = {}, {}
-        for mt in (2, 3):
-            w2_codes[mt] = late_codes[:, mt * P : (mt + 1) * P]
-            w2_scales[mt] = late_scales[:, mt * P : (mt + 1) * P]
-
-        def token_cols(j0, j1):
-            shift = 0 if j0 < HALF else HALF
-            return slice(j0 + shift, j1 + shift)
 
         def round_w2(mt):
             lo = (mt % 2) * P
-            dest = early_bf if mt < 2 else late_bf
-            nc.scalar.copy(
-                dest[:, mt * P : (mt + 1) * P, :].rearrange("p (c i) j -> p c j i", i=4),
-                w2_raw[mt // 2][:, :, lo : lo + P].rearrange("p j (c i) -> p c j i", i=4),
+            nc.gpsimd.tensor_scalar(
+                w2_bf[:, mt * P : (mt + 1) * P, :],
+                w2_raw[mt // 2][:, :, lo : lo + P].rearrange("p j c -> p c j"),
+                1.0,
+                0.0,
+                MULT,
+                ADD,
             )
 
-        def quantize_early(mt, slot):
-            codes = keep.tile([P, P], U32, name="w2_codes%d" % mt, tag=slot, align_bytes=64)
-            w2_codes[mt] = codes[:]
-            w2_scales[mt] = early_scales[:, mt * P : (mt + 1) * P]
+        def quantize_w2(mt0, mt1, slot):
+            codes = keep.tile([P, (mt1 - mt0) * P], U32, name="w2_codes%d" % mt0, tag=slot, align_bytes=64)
+            for mt in range(mt0, mt1):
+                w2_codes[mt] = codes[:, (mt - mt0) * P : (mt - mt0 + 1) * P]
+                w2_scales[mt] = w2_scale_bytes[:, mt * P : (mt + 1) * P]
             nc.vector.quantize_mx(
                 out=codes[:].bitcast(FP8X4),
-                scales=w2_scales[mt],
-                in_=early_bf[:, mt * P : (mt + 1) * P, :].rearrange("p n j -> p (n j)"),
+                scales=w2_scale_bytes[:, mt0 * P : mt1 * P],
+                in_=w2_bf[:, mt0 * P : mt1 * P, :].rearrange("p n j -> p (n j)"),
             )
 
-        def quantize_late(b0, b1):
+        def quantize_z(j0, j1):
             nc.vector.quantize_mx(
-                out=late_codes[:, b0 * P : b1 * P].bitcast(FP8X4),
-                scales=late_scales[:, b0 * P : b1 * P],
-                in_=late_bf[:, b0 * P : b1 * P, :].rearrange("p n j -> p (n j)"),
+                out=z_codes[:, j0:j1].bitcast(FP8X4),
+                scales=z_scales[:, j0:j1],
+                in_=z_bf[:, j0:j1, :].rearrange("p n j -> p (n j)"),
             )
 
         def pair_views(t, j0, j1):
             pair = z[t][:].rearrange("p (s n) -> p n s", s=2)
-            return late_bf[:, token_cols(j0, j1), t : t + 2], pair[:, j0:j1, :]
+            return z_bf[:, j0:j1, t : t + 2], pair[:, j0:j1, :]
 
-        for t, b, bank in odd_blocks:
-            if (b % 2 == 1) if t == 1 else (b == 0):
-                nc.vector.tensor_copy(z[t][:, b * P : (b + 1) * P], bank[:])
-            else:
-                nc.scalar.copy(z[t][:, b * P : (b + 1) * P], bank[:])
-        fetch(1)
-        fetch(3)
-        activate(1)
+        last_block = S // P - 1
+        for b in range(S // P):
+            bank = first_product(1, b * P, (b + 1) * P)
+            nc.scalar.activation(relu1[:, b * P : (b + 1) * P], bank[:], RELU)
+            if b < last_block:
+                nc.vector.tensor_copy(z[1][:, b * P : (b + 1) * P], bank[:])
+        half_cols = V // LIST_COL // 2
+        nc.scalar.activation(act[1][:, 0 : V // 2], relu1[:].indirect(src_t[:, 0:half_cols]), COPY)
+        nc.vector.tensor_copy(out=act[1][:, V // 2 : V], in_=relu1[:].indirect(src_t[:, half_cols : 2 * half_cols]))
+        nc.scalar.copy(z[1][:, last_block * P : S], bank[:])
+        nc.vector.tensor_copy(z[3][:, 0:HALF], first_product(3, 0, HALF)[:])
         deliver(1)
-        nc.scalar.copy(z[0][:, 0:S], first_product(0, 0, S)[:])
-        fetch(0)
+        nc.scalar.copy(z[3][:, HALF:S], first_product(3, HALF, S)[:])
+        bank0 = first_product(0, 0, S)
+        nc.scalar.copy(z[0][:, 0:P], bank0[:, 0:P])
+        fetch(3)
+        nc.scalar.copy(z[0][:, P:HALF], bank0[:, P:HALF])
         activate(3)
         deliver(3)
-        nc.scalar.copy(z[2][:, 0:S], first_product(2, 0, S)[:])
-        fetch(2)
-        round_w2(0)
-        round_w2(1)
-        activate(0)
+        nc.scalar.copy(z[0][:, HALF:S], bank0[:, HALF:S])
+        bank2 = first_product(2, 0, S)
+        nc.scalar.copy(z[2][:, 0:HALF], bank2[:, 0:HALF])
+        fetch(0)
         join(1)
+        nc.scalar.copy(z[2][:, HALF:S], bank2[:, HALF:S])
+        activate(0)
         deliver(0)
-        round_w2(2)
+        fetch(2)
         join(3)
         activate(2)
-        round_w2(3)
         deliver(2)
-        quantize_early(0, "slot_even")
+        for mt in range(N // P):
+            round_w2(mt)
+        quantize_w2(0, 1, "slot_z3")
         for j0, j1 in ((0, P), (P, HALF), (HALF, S)):
             nc.scalar.copy(*pair_views(0, j0, j1))
 
@@ -224,8 +231,8 @@ def tile_picked_deliver_relu_p_kernel(
                 out=dest,
                 lhsT=w2_codes[mt].bitcast(FP8X4),
                 lhsT_scale=w2_scales[mt],
-                rhs=late_codes[:, token_cols(j0, j1)].bitcast(FP8X4),
-                rhs_scale=late_scales[:, token_cols(j0, j1)],
+                rhs=z_codes[:, j0:j1].bitcast(FP8X4),
+                rhs_scale=z_scales[:, j0:j1],
                 start=True,
                 stop=True,
             )
@@ -255,14 +262,16 @@ def tile_picked_deliver_relu_p_kernel(
         nc.vector.tensor_copy(*pair_views(2, 0, P))
         for b in range(1, S // P):
             nc.scalar.copy(*pair_views(2, b * P, (b + 1) * P))
-        quantize_early(1, "slot_act")
-        for b0, b1 in ((0, 1), (1, 3), (3, 5), (5, 6)):
-            quantize_late(b0, b1)
+        quantize_w2(1, 2, "slot_act")
+        quantize_z(0, P)
+        quantize_w2(2, 4, "slot_z0")
+        for b in range(1, S // P):
+            quantize_z(b * P, (b + 1) * P)
         output_piece(0, 1, 0, P, False)
         output_piece(1, 2, 0, P, False)
-        output_piece(0, 2, P, HALF, False)
-        output_piece(2, 3, 0, HALF, True)
-        output_piece(3, 4, 0, HALF, False)
+        output_piece(2, 4, 0, P, False)
+        output_piece(0, 2, P, HALF, True)
+        output_piece(2, 4, P, HALF, False)
         for mt in range(3):
             output_piece(mt, mt + 1, HALF, S, mt % 2 == 0)
         last = result_tile(3, 4, HALF, S)

@@ -26,6 +26,7 @@ SPREAD = 8
 BANKS = 8
 X_FIRST = 896
 W1_LAST = 96
+GOT_AT = 512
 
 
 def tile_picked_deliver_relu_p_kernel(
@@ -34,6 +35,7 @@ def tile_picked_deliver_relu_p_kernel(
     nc = tc.nc
     with ExitStack() as ctx:
         keep = ctx.enter_context(tc.tile_pool(name="keep", bufs=1))
+        laid = ctx.enter_context(tc.tile_pool(name="laid", bufs=1))
         psum = ctx.enter_context(tc.psum_pool(name="psum", bufs=BANKS))
 
         offs_t = keep.tile([P, S // LIST_COL], U16, name="offs_t")
@@ -130,8 +132,9 @@ def tile_picked_deliver_relu_p_kernel(
             return bank
 
         got, act = {}, {}
-        for t, slot in ((3, "got3"), (0, "slot_even"), (2, "slot_even")):
-            got[t] = keep.tile([P, V], F32, name="got%d" % t, tag=slot, align_bytes=64)
+        got[3] = keep.tile([P, V], F32, name="got3", align_bytes=64)
+        for t in (0, 2):
+            got[t] = laid.tile([P, V], F32, name="got%d" % t, offset=GOT_AT, align_bytes=64)
         for t, slot in ((1, "act1"), (3, "slot_act"), (0, "act0"), (2, "slot_act")):
             act[t] = keep.tile([P, V], F32, name="act%d" % t, tag=slot, align_bytes=64)
 
@@ -149,33 +152,24 @@ def tile_picked_deliver_relu_p_kernel(
         def join(t):
             nc.gpsimd.tensor_scalar(z[t - 1][:, S : 2 * S], z[t][:], 1.0, 0.0, MULT, ADD)
 
-        w2_bf = keep.tile([P, N, PACK], BF16, name="w2_bf", tag="slot_w1bf0", align_bytes=64)
+        w2_bf_early = keep.tile([P, N - P, PACK], BF16, name="w2_bf_early", tag="slot_w1bf0", align_bytes=64)
+        w2_bf_last = laid.tile([P, P, PACK], BF16, name="w2_bf_last", offset=0, align_bytes=64)
+        w2_bf = [w2_bf_early[:, mt * P : (mt + 1) * P, :] for mt in range(3)] + [w2_bf_last[:]]
         w2_scale_bytes = keep.tile([P, N], U8, name="w2_scale_bytes", align_bytes=64)
-        z_bf = keep.tile([P, S, PACK], BF16, name="z_bf", tag="slot_even", align_bytes=64)
+        z_bf = laid.tile([P, S, PACK], BF16, name="z_bf", offset=2 * GOT_AT, align_bytes=64)
         z_codes = keep.tile([P, S], U32, name="z_codes", align_bytes=64)
         z_scales = keep.tile([P, S], U8, name="z_scales", align_bytes=64)
         w2_codes, w2_scales = {}, {}
 
-        def round_w2(mt):
+        def w2_views(mt):
             lo = (mt % 2) * P
-            nc.gpsimd.tensor_scalar(
-                w2_bf[:, mt * P : (mt + 1) * P, :],
-                w2_raw[mt // 2][:, :, lo : lo + P].rearrange("p j c -> p c j"),
-                1.0,
-                0.0,
-                MULT,
-                ADD,
-            )
+            return w2_bf[mt], w2_raw[mt // 2][:, :, lo : lo + P].rearrange("p j c -> p c j")
 
-        def quantize_w2(mt0, mt1, slot):
-            codes = keep.tile([P, (mt1 - mt0) * P], U32, name="w2_codes%d" % mt0, tag=slot, align_bytes=64)
-            for mt in range(mt0, mt1):
-                w2_codes[mt] = codes[:, (mt - mt0) * P : (mt - mt0 + 1) * P]
-                w2_scales[mt] = w2_scale_bytes[:, mt * P : (mt + 1) * P]
+        def quantize_w2(mt, codes):
+            w2_codes[mt] = codes
+            w2_scales[mt] = w2_scale_bytes[:, mt * P : (mt + 1) * P]
             nc.vector.quantize_mx(
-                out=codes[:].bitcast(FP8X4),
-                scales=w2_scale_bytes[:, mt0 * P : mt1 * P],
-                in_=w2_bf[:, mt0 * P : mt1 * P, :].rearrange("p n j -> p (n j)"),
+                out=codes.bitcast(FP8X4), scales=w2_scales[mt], in_=w2_bf[mt].rearrange("p n j -> p (n j)")
             )
 
         def quantize_z(j0, j1):
@@ -220,9 +214,13 @@ def tile_picked_deliver_relu_p_kernel(
         join(3)
         activate(2)
         deliver(2)
-        for mt in range(N // P):
-            round_w2(mt)
-        quantize_w2(0, 1, "slot_z3")
+        for mt in range(N // P - 1):
+            nc.gpsimd.tensor_scalar(*w2_views(mt), 1.0, 0.0, MULT, ADD)
+        nc.scalar.copy(*w2_views(3))
+        codes0 = keep.tile([P, P], U32, name="codes0", tag="slot_z3", align_bytes=64)
+        codes1 = keep.tile([P, P], U32, name="codes1", tag="slot_act", align_bytes=64)
+        codes23 = keep.tile([P, HALF], U32, name="codes23", tag="slot_z0", align_bytes=64)
+        quantize_w2(0, codes0[:])
         for j0, j1 in ((0, P), (P, HALF), (HALF, S)):
             nc.scalar.copy(*pair_views(0, j0, j1))
 
@@ -262,9 +260,10 @@ def tile_picked_deliver_relu_p_kernel(
         nc.vector.tensor_copy(*pair_views(2, 0, P))
         for b in range(1, S // P):
             nc.scalar.copy(*pair_views(2, b * P, (b + 1) * P))
-        quantize_w2(1, 2, "slot_act")
+        quantize_w2(1, codes1[:])
         quantize_z(0, P)
-        quantize_w2(2, 4, "slot_z0")
+        quantize_w2(2, codes23[:, 0:P])
+        quantize_w2(3, codes23[:, P:HALF])
         for b in range(1, S // P):
             quantize_z(b * P, (b + 1) * P)
         output_piece(0, 1, 0, P, False)

@@ -45,7 +45,7 @@ def tile_picked_deliver_relu_p_kernel(
         xs = keep.tile([P, T], U8, name="xs", tag="slot_xs", align_bytes=64)
         w1_parts = ((0, 0, P), (1, 0, W1_LAST), (1, W1_LAST, P))
         w1_raw = [
-            keep.tile([P, 2, PACK * (m1 - m0)], F32, name="w1_raw%d" % i, align_bytes=64)
+            keep.tile([P, 2, PACK * (m1 - m0)], F32, name="w1_raw%d" % i, tag="slot_w1raw%d" % i, align_bytes=64)
             for i, (u, m0, m1) in enumerate(w1_parts)
         ]
 
@@ -98,12 +98,13 @@ def tile_picked_deliver_relu_p_kernel(
         nc.sync.dma_start(src_t[:], src)
         nc.sync.dma_start(dst_t[:], dst)
         nc.vector.tensor_copy(out=xw_g[:], in_=xw[:].indirect(offs_t[:]))
-        w2_raw = []
-        for u, slot in enumerate(("slot_xs", "slot_xw")):
-            w2_raw.append(keep.tile([P, PACK, HALF], F32, name="w2_raw%d" % u, tag=slot, align_bytes=64))
-            nc.sync.dma_start(
-                out=w2_raw[u][:], in_=w2.rearrange("(p j) c -> p j c", j=PACK)[:, :, u * HALF : (u + 1) * HALF]
-            )
+        w2_rows = w2.rearrange("(p j) c -> p j c", j=PACK)
+        w2_raw = {}
+        for mt0, mt1, slot in ((0, 2, "slot_xs"), (2, 3, "slot_xw"), (3, 4, "slot_w1raw0")):
+            raw = keep.tile([P, PACK, (mt1 - mt0) * P], F32, name="w2_raw%d" % mt0, tag=slot, align_bytes=64)
+            nc.sync.dma_start(out=raw[:], in_=w2_rows[:, :, mt0 * P : mt1 * P])
+            for mt in range(mt0, mt1):
+                w2_raw[mt] = raw[:, :, (mt - mt0) * P : (mt - mt0 + 1) * P]
 
         nc.vector.tensor_copy(*w1_views(1, 0))
         nc.scalar.activation(*w1_views(0, 0), COPY)
@@ -162,8 +163,7 @@ def tile_picked_deliver_relu_p_kernel(
         w2_codes, w2_scales = {}, {}
 
         def w2_views(mt):
-            lo = (mt % 2) * P
-            return w2_bf[mt], w2_raw[mt // 2][:, :, lo : lo + P].rearrange("p j c -> p c j")
+            return w2_bf[mt], w2_raw[mt].rearrange("p j c -> p c j")
 
         def quantize_w2(mt, codes):
             w2_codes[mt] = codes
@@ -224,7 +224,9 @@ def tile_picked_deliver_relu_p_kernel(
         for j0, j1 in ((0, P), (P, HALF), (HALF, S)):
             nc.scalar.copy(*pair_views(0, j0, j1))
 
-        def second_product(mt, j0, j1, dest):
+        out_rows = out.rearrange("(mt p) j -> p mt j", p=P)
+
+        def second_product(dest, mt, j0, j1):
             nc.tensor.matmul_mx(
                 out=dest,
                 lhsT=w2_codes[mt].bitcast(FP8X4),
@@ -235,27 +237,19 @@ def tile_picked_deliver_relu_p_kernel(
                 stop=True,
             )
 
-        out_rows = out.rearrange("(mt p) j -> p mt j", p=P)
+        def new_bank(*shape):
+            return psum.tile([P, *shape], F32, name="bank", tag="bank")
 
-        def product_part(res, mt0, mt1, j0, j1, on_vector):
-            bank = psum.tile([P, mt1 - mt0, j1 - j0], F32, name="bank", tag="bank")
-            for mt in range(mt0, mt1):
-                second_product(mt, j0, j1, bank[:, mt - mt0, :])
+        def empty(dest, bank, on_vector):
             if on_vector:
-                nc.vector.tensor_copy(out=res, in_=bank[:])
+                nc.vector.tensor_copy(out=dest, in_=bank)
             else:
-                nc.scalar.copy(res, bank[:])
+                nc.scalar.copy(dest, bank)
 
-        def result_tile(mt0, mt1, j0, j1):
-            return keep.tile([P, mt1 - mt0, j1 - j0], F32, name="res%d_%d" % (mt0, j0), align_bytes=64)
+        res = keep.tile([P, N // P, S], F32, name="res", align_bytes=64)
 
-        def store(res, mt0, mt1, j0, j1):
-            nc.sync.dma_start(out=out_rows[:, mt0:mt1, j0:j1], in_=res[:])
-
-        def output_piece(mt0, mt1, j0, j1, on_vector):
-            res = result_tile(mt0, mt1, j0, j1)
-            product_part(res[:], mt0, mt1, j0, j1, on_vector)
-            store(res, mt0, mt1, j0, j1)
+        def store(mt, j0, j1):
+            nc.sync.dma_start(out=out_rows[:, mt, j0:j1], in_=res[:, mt, j0:j1])
 
         nc.vector.tensor_copy(*pair_views(2, 0, P))
         for b in range(1, S // P):
@@ -263,17 +257,33 @@ def tile_picked_deliver_relu_p_kernel(
         quantize_w2(1, codes1[:])
         quantize_z(0, P)
         quantize_w2(2, codes23[:, 0:P])
+        quantize_z(P, HALF)
         quantize_w2(3, codes23[:, P:HALF])
-        for b in range(1, S // P):
+        for b in range(2, S // P):
             quantize_z(b * P, (b + 1) * P)
-        output_piece(0, 1, 0, P, False)
-        output_piece(1, 2, 0, P, False)
-        output_piece(2, 4, 0, P, False)
-        output_piece(0, 2, P, HALF, True)
-        output_piece(2, 4, P, HALF, False)
-        for mt in range(3):
-            output_piece(mt, mt + 1, HALF, S, mt % 2 == 0)
-        last = result_tile(3, 4, HALF, S)
-        product_part(last[:, :, 0:P], 3, 4, HALF, HALF + P, False)
-        product_part(last[:, :, P:HALF], 3, 4, HALF + P, S, True)
-        store(last, 3, 4, HALF, S)
+        for mt in (0, 1):
+            bank = new_bank(P)
+            second_product(bank[:], mt, 0, P)
+            empty(res[:, mt, 0:P], bank[:], False)
+            store(mt, 0, P)
+        for mt in (2, 3):
+            bank = new_bank(HALF)
+            for b in range(2):
+                second_product(bank[:, b * P : (b + 1) * P], mt, b * P, (b + 1) * P)
+            empty(res[:, mt, 0:HALF], bank[:], mt == 3)
+            store(mt, 0, HALF)
+        for mt in (0, 1):
+            for j0, j1 in ((P, HALF), (HALF, S)):
+                bank = new_bank(j1 - j0)
+                second_product(bank[:], mt, j0, j1)
+                empty(res[:, mt, j0:j1], bank[:], mt == 0 and j0 == HALF)
+            store(mt, P, S)
+        bank = new_bank(HALF)
+        second_product(bank[:], 2, HALF, S)
+        empty(res[:, 2, HALF:S], bank[:], True)
+        store(2, HALF, S)
+        for b in (2, 3):
+            bank = new_bank(P)
+            second_product(bank[:], 3, b * P, (b + 1) * P)
+            empty(res[:, 3, b * P : (b + 1) * P], bank[:], b == 3)
+        store(3, HALF, S)

@@ -27,6 +27,7 @@ BANKS = 8
 X_FIRST = 896
 W1_LAST = 96
 GOT_AT = 512
+WARM_PASSES, WARM_M = 3, 32
 
 
 def tile_picked_deliver_relu_p_kernel(
@@ -71,10 +72,12 @@ def tile_picked_deliver_relu_p_kernel(
         nc.vector.memset(xs_g[:].bitcast(I32), 0)
 
         w1_codes, w1_scales, w1_bf = {}, {}, {}
+        w1_all_codes = keep.tile([P, H], U32, name="w1_all_codes", align_bytes=64)
+        w1_all_scales = keep.tile([P, H], U8, name="w1_all_scales", align_bytes=64)
         for e in (1, 0):
             w1_bf[e] = keep.tile([P, 2, P, PACK], BF16, name="w1_bf%d" % e, tag="slot_w1bf%d" % e, align_bytes=64)
-            w1_codes[e] = keep.tile([P, 2 * P], U32, name="w1_codes%d" % e, align_bytes=64)
-            w1_scales[e] = keep.tile([P, 2 * P], U8, name="w1_scales%d" % e, align_bytes=64)
+            w1_codes[e] = w1_all_codes[:, e * HALF : (e + 1) * HALF]
+            w1_scales[e] = w1_all_scales[:, e * HALF : (e + 1) * HALF]
 
         def w1_views(e, i):
             u, m0, m1 = w1_parts[i]
@@ -213,14 +216,26 @@ def tile_picked_deliver_relu_p_kernel(
         fetch(2)
         join(3)
         activate(2)
-        deliver(2)
         for mt in range(N // P - 1):
             nc.gpsimd.tensor_scalar(*w2_views(mt), 1.0, 0.0, MULT, ADD)
+        codes01 = keep.tile([P, HALF], U32, name="codes01", tag="slot_z3", align_bytes=64)
+        quantize_w2(0, codes01[:, 0:P])
+        deliver(2)
+        for warm in range(WARM_PASSES):
+            idle = psum.tile([WARM_M, H], F32, name="bank", tag="bank")
+            nc.tensor.matmul_mx(
+                out=idle[:],
+                lhsT=w2_codes[0][:, 0:WARM_M].bitcast(FP8X4),
+                lhsT_scale=w2_scales[0][:, 0:WARM_M],
+                rhs=w1_all_codes[:].bitcast(FP8X4),
+                rhs_scale=w1_all_scales[:],
+                start=True,
+                stop=True,
+            )
         nc.scalar.copy(*w2_views(3))
-        codes0 = keep.tile([P, P], U32, name="codes0", tag="slot_z3", align_bytes=64)
-        codes1 = keep.tile([P, P], U32, name="codes1", tag="slot_act", align_bytes=64)
-        codes23 = keep.tile([P, HALF], U32, name="codes23", tag="slot_z0", align_bytes=64)
-        quantize_w2(0, codes0[:])
+        codes2 = keep.tile([P, P], U32, name="codes2", tag="slot_act", align_bytes=64)
+        codes3 = keep.tile([P, P], U32, name="codes3", tag="slot_z0", align_bytes=64)
+        quantize_w2(1, codes01[:, P:HALF])
         for j0, j1 in ((0, P), (P, HALF), (HALF, S)):
             nc.scalar.copy(*pair_views(0, j0, j1))
 
@@ -251,14 +266,13 @@ def tile_picked_deliver_relu_p_kernel(
         def store(mt, j0, j1):
             nc.sync.dma_start(out=out_rows[:, mt, j0:j1], in_=res[:, mt, j0:j1])
 
-        nc.vector.tensor_copy(*pair_views(2, 0, P))
-        for b in range(1, S // P):
-            nc.scalar.copy(*pair_views(2, b * P, (b + 1) * P))
-        quantize_w2(1, codes1[:])
+        for b in range(S // P):
+            engine_copy = nc.vector.tensor_copy if b < 2 else nc.scalar.copy
+            engine_copy(*pair_views(2, b * P, (b + 1) * P))
         quantize_z(0, P)
-        quantize_w2(2, codes23[:, 0:P])
+        quantize_w2(2, codes2[:])
         quantize_z(P, HALF)
-        quantize_w2(3, codes23[:, P:HALF])
+        quantize_w2(3, codes3[:])
         for b in range(2, S // P):
             quantize_z(b * P, (b + 1) * P)
         for mt in (0, 1):

from contextlib import ExitStack

import concourse.mybir as mybir

K, T, S, V, H, N = 512, 2048, 512, 256, 512, 512
FLOPS = 2 * K * H * S + 2 * H * N * S

F32 = mybir.dt.float32
BF16 = mybir.dt.bfloat16
I32 = mybir.dt.int32
U32 = mybir.dt.uint32
U16 = mybir.dt.uint16
U8 = mybir.dt.uint8
FP8X4 = mybir.dt.float8_e4m3fn_x4
COPY = mybir.ActivationFunctionType.Copy
RELU = mybir.ActivationFunctionType.Relu
MULT = mybir.AluOpType.mult
ADD = mybir.AluOpType.add

P = 128
PACK = 4
HALF = 256
LIST_COL = 16
QUADRANT = 32
SPREAD = 8
BANKS = 8
X_FIRST = 896
W1_LAST = 96
GOT_AT = 512
WARM_PASSES, WARM_M = 3, 32


def tile_picked_deliver_relu_p_kernel(
    tc, x_words, x_scales, w1, w2, offs, src, dst, out
):
    nc = tc.nc
    with ExitStack() as ctx:
        keep = ctx.enter_context(tc.tile_pool(name="keep", bufs=1))
        laid = ctx.enter_context(tc.tile_pool(name="laid", bufs=1))
        psum = ctx.enter_context(tc.psum_pool(name="psum", bufs=BANKS))

        offs_t = keep.tile([P, S // LIST_COL], U16, name="offs_t")
        src_t = keep.tile([P, V // LIST_COL], U16, name="src_t")
        dst_t = keep.tile([P, V // LIST_COL], U16, name="dst_t")
        xw = keep.tile([P, T], U32, name="xw", tag="slot_xw", align_bytes=64)
        xs = keep.tile([P, T], U8, name="xs", tag="slot_xs", align_bytes=64)
        w1_parts = ((0, 0, P), (1, 0, W1_LAST), (1, W1_LAST, P))
        w1_raw = [
            keep.tile([P, 2, PACK * (m1 - m0)], F32, name="w1_raw%d" % i, tag="slot_w1raw%d" % i, align_bytes=64)
            for i, (u, m0, m1) in enumerate(w1_parts)
        ]

        nc.vector.memset(xs[:].bitcast(I32), 0)
        w1_rows = w1.rearrange("(p j) c -> p j c", j=PACK)
        x_cols = x_words[0].rearrange("p n t -> p (n t)").bitcast(I32)
        nc.sync.dma_start(out=xw[:, 0:X_FIRST].bitcast(I32), in_=x_cols[:, 0:X_FIRST])
        nc.sync.dma_start(offs_t[:], offs)
        nc.sync.dma_start(out=xs[0:P:SPREAD, :].bitcast(I32), in_=x_scales[0].bitcast(I32))
        nc.sync.dma_start(out=xw[:, X_FIRST:T].bitcast(I32), in_=x_cols[:, X_FIRST:T])
        for i, (u, m0, m1) in enumerate(w1_parts):
            nc.sync.dma_start(out=w1_raw[i][:], in_=w1_rows[:, 2 * u : 2 * u + 2, PACK * m0 : PACK * m1])

        z = {}
        for t in (1, 3):
            z[t] = keep.tile([P, S], F32, name="z%d" % t, tag="slot_z%d" % t, align_bytes=64)
        for t in (0, 2):
            z[t] = keep.tile([P, 2 * S], F32, name="z%d" % t, tag="slot_z%d" % t, align_bytes=64)
        nc.vector.memset(z[0][:, S : 2 * S], 0.0)
        nc.scalar.activation(z[2][:, S : 2 * S], z[0][:, S : 2 * S], COPY)

        xs_g = keep.tile([P, S], U8, name="xs_g", align_bytes=64)
        nc.vector.memset(xs_g[:].bitcast(I32), 0)

        w1_codes, w1_scales, w1_bf = {}, {}, {}
        w1_all_codes = keep.tile([P, H], U32, name="w1_all_codes", align_bytes=64)
        w1_all_scales = keep.tile([P, H], U8, name="w1_all_scales", align_bytes=64)
        for e in (1, 0):
            w1_bf[e] = keep.tile([P, 2, P, PACK], BF16, name="w1_bf%d" % e, tag="slot_w1bf%d" % e, align_bytes=64)
            w1_codes[e] = w1_all_codes[:, e * HALF : (e + 1) * HALF]
            w1_scales[e] = w1_all_scales[:, e * HALF : (e + 1) * HALF]

        def w1_views(e, i):
            u, m0, m1 = w1_parts[i]
            cols = w1_raw[i][:].rearrange("p j (m s e) -> p e m j s", s=2, e=2)
            return w1_bf[e][:, :, m0:m1, 2 * u : 2 * u + 2].rearrange("p s m j -> p m j s"), cols[:, e]

        def quantize_w1(e, s0, s1):
            nc.vector.quantize_mx(
                out=w1_codes[e][:, s0 * P : s1 * P].bitcast(FP8X4),
                scales=w1_scales[e][:, s0 * P : s1 * P],
                in_=w1_bf[e][:, s0:s1].rearrange("p s m j -> p (s m j)"),
            )

        xw_g = keep.tile([P, S], U32, name="xw_g", align_bytes=64)
        xs_spread = keep.tile([P, S], U8, name="xs_spread", align_bytes=64)
        nc.vector.tensor_copy(out=xs_spread[:], in_=xs[:].indirect(offs_t[:]))
        for r in range(QUADRANT // SPREAD):
            nc.sync.dma_start(
                out=xs_g[r:P:QUADRANT, :].bitcast(I32), in_=xs_spread[SPREAD * r : P : QUADRANT, :].bitcast(I32)
            )
        nc.sync.dma_start(src_t[:], src)
        nc.sync.dma_start(dst_t[:], dst)
        nc.vector.tensor_copy(out=xw_g[:], in_=xw[:].indirect(offs_t[:]))
        w2_rows = w2.rearrange("(p j) c -> p j c", j=PACK)
        w2_raw = {}
        for mt0, mt1, slot in ((0, 2, "slot_xs"), (2, 3, "slot_xw"), (3, 4, "slot_w1raw0")):
            raw = keep.tile([P, PACK, (mt1 - mt0) * P], F32, name="w2_raw%d" % mt0, tag=slot, align_bytes=64)
            nc.sync.dma_start(out=raw[:], in_=w2_rows[:, :, mt0 * P : mt1 * P])
            for mt in range(mt0, mt1):
                w2_raw[mt] = raw[:, :, (mt - mt0) * P : (mt - mt0 + 1) * P]

        nc.vector.tensor_copy(*w1_views(1, 0))
        nc.scalar.activation(*w1_views(0, 0), COPY)
        nc.vector.tensor_copy(*w1_views(1, 1))
        last_out, last_in = w1_views(1, 2)
        for s in range(2):
            nc.vector.tensor_copy(last_out[:, :, :, s], last_in[:, :, :, s])
        for i in (1, 2):
            nc.scalar.activation(*w1_views(0, i), COPY)
        quantize_w1(1, 0, 1)
        quantize_w1(1, 1, 2)
        quantize_w1(0, 0, 2)

        def first_product(t, j0, j1):
            bank = psum.tile([P, j1 - j0], F32, name="bank", tag="bank")
            m_cols = slice((t // 2) * P, (t // 2 + 1) * P)
            nc.tensor.matmul_mx(
                out=bank[:],
                lhsT=w1_codes[t % 2][:, m_cols].bitcast(FP8X4),
                lhsT_scale=w1_scales[t % 2][:, m_cols],
                rhs=xw_g[:, j0:j1].bitcast(FP8X4),
                rhs_scale=xs_g[:, j0:j1],
                start=True,
                stop=True,
            )
            return bank

        got, act = {}, {}
        got[3] = keep.tile([P, V], F32, name="got3", align_bytes=64)
        for t in (0, 2):
            got[t] = laid.tile([P, V], F32, name="got%d" % t, offset=GOT_AT, align_bytes=64)
        for t, slot in ((1, "act1"), (3, "slot_act"), (0, "act0"), (2, "slot_act")):
            act[t] = keep.tile([P, V], F32, name="act%d" % t, tag=slot, align_bytes=64)

        relu1 = keep.tile([P, S], F32, name="relu1", align_bytes=64)

        def fetch(t):
            nc.scalar.activation(got[t][:], z[t][:].indirect(src_t[:]), COPY)

        def activate(t):
            nc.scalar.activation(act[t][:], got[t][:], RELU)

        def deliver(t):
            nc.vector.tensor_copy(out=z[t][:].indirect(dst_t[:]), in_=act[t][:])

        def join(t):
            nc.gpsimd.tensor_scalar(z[t - 1][:, S : 2 * S], z[t][:], 1.0, 0.0, MULT, ADD)

        w2_bf_early = keep.tile([P, N - P, PACK], BF16, name="w2_bf_early", tag="slot_w1bf0", align_bytes=64)
        w2_bf_last = laid.tile([P, P, PACK], BF16, name="w2_bf_last", offset=0, align_bytes=64)
        w2_bf = [w2_bf_early[:, mt * P : (mt + 1) * P, :] for mt in range(3)] + [w2_bf_last[:]]
        w2_scale_bytes = keep.tile([P, N], U8, name="w2_scale_bytes", align_bytes=64)
        z_bf = laid.tile([P, S, PACK], BF16, name="z_bf", offset=2 * GOT_AT, align_bytes=64)
        z_codes = keep.tile([P, S], U32, name="z_codes", align_bytes=64)
        z_scales = keep.tile([P, S], U8, name="z_scales", align_bytes=64)
        w2_codes, w2_scales = {}, {}

        def w2_views(mt):
            return w2_bf[mt], w2_raw[mt].rearrange("p j c -> p c j")

        def quantize_w2(mt, codes):
            w2_codes[mt] = codes
            w2_scales[mt] = w2_scale_bytes[:, mt * P : (mt + 1) * P]
            nc.vector.quantize_mx(
                out=codes.bitcast(FP8X4), scales=w2_scales[mt], in_=w2_bf[mt].rearrange("p n j -> p (n j)")
            )

        def quantize_z(j0, j1):
            nc.vector.quantize_mx(
                out=z_codes[:, j0:j1].bitcast(FP8X4),
                scales=z_scales[:, j0:j1],
                in_=z_bf[:, j0:j1, :].rearrange("p n j -> p (n j)"),
            )

        def pair_views(t, j0, j1):
            pair = z[t][:].rearrange("p (s n) -> p n s", s=2)
            return z_bf[:, j0:j1, t : t + 2], pair[:, j0:j1, :]

        last_block = S // P - 1
        for b in range(S // P):
            bank = first_product(1, b * P, (b + 1) * P)
            nc.scalar.activation(relu1[:, b * P : (b + 1) * P], bank[:], RELU)
            if b < last_block:
                nc.vector.tensor_copy(z[1][:, b * P : (b + 1) * P], bank[:])
        half_cols = V // LIST_COL // 2
        nc.scalar.activation(act[1][:, 0 : V // 2], relu1[:].indirect(src_t[:, 0:half_cols]), COPY)
        nc.vector.tensor_copy(out=act[1][:, V // 2 : V], in_=relu1[:].indirect(src_t[:, half_cols : 2 * half_cols]))
        nc.scalar.copy(z[1][:, last_block * P : S], bank[:])
        nc.vector.tensor_copy(z[3][:, 0:HALF], first_product(3, 0, HALF)[:])
        deliver(1)
        nc.scalar.copy(z[3][:, HALF:S], first_product(3, HALF, S)[:])
        bank0 = first_product(0, 0, S)
        nc.scalar.copy(z[0][:, 0:P], bank0[:, 0:P])
        fetch(3)
        nc.scalar.copy(z[0][:, P:HALF], bank0[:, P:HALF])
        activate(3)
        deliver(3)
        nc.scalar.copy(z[0][:, HALF:S], bank0[:, HALF:S])
        bank2 = first_product(2, 0, S)
        nc.scalar.copy(z[2][:, 0:HALF], bank2[:, 0:HALF])
        fetch(0)
        join(1)
        nc.scalar.copy(z[2][:, HALF:S], bank2[:, HALF:S])
        activate(0)
        deliver(0)
        fetch(2)
        join(3)
        activate(2)
        for mt in range(N // P - 1):
            nc.gpsimd.tensor_scalar(*w2_views(mt), 1.0, 0.0, MULT, ADD)
        codes01 = keep.tile([P, HALF], U32, name="codes01", tag="slot_z3", align_bytes=64)
        quantize_w2(0, codes01[:, 0:P])
        deliver(2)
        for warm in range(WARM_PASSES):
            idle = psum.tile([WARM_M, H], F32, name="bank", tag="bank")
            nc.tensor.matmul_mx(
                out=idle[:],
                lhsT=w2_codes[0][:, 0:WARM_M].bitcast(FP8X4),
                lhsT_scale=w2_scales[0][:, 0:WARM_M],
                rhs=w1_all_codes[:].bitcast(FP8X4),
                rhs_scale=w1_all_scales[:],
                start=True,
                stop=True,
            )
        nc.scalar.copy(*w2_views(3))
        codes2 = keep.tile([P, P], U32, name="codes2", tag="slot_act", align_bytes=64)
        codes3 = keep.tile([P, P], U32, name="codes3", tag="slot_z0", align_bytes=64)
        quantize_w2(1, codes01[:, P:HALF])
        for j0, j1 in ((0, P), (P, HALF), (HALF, S)):
            nc.scalar.copy(*pair_views(0, j0, j1))

        out_rows = out.rearrange("(mt p) j -> p mt j", p=P)

        def second_product(dest, mt, j0, j1):
            nc.tensor.matmul_mx(
                out=dest,
                lhsT=w2_codes[mt].bitcast(FP8X4),
                lhsT_scale=w2_scales[mt],
                rhs=z_codes[:, j0:j1].bitcast(FP8X4),
                rhs_scale=z_scales[:, j0:j1],
                start=True,
                stop=True,
            )

        def new_bank(*shape):
            return psum.tile([P, *shape], F32, name="bank", tag="bank")

        def empty(dest, bank, on_vector):
            if on_vector:
                nc.vector.tensor_copy(out=dest, in_=bank)
            else:
                nc.scalar.copy(dest, bank)

        res = keep.tile([P, N // P, S], F32, name="res", align_bytes=64)

        def store(mt, j0, j1):
            nc.sync.dma_start(out=out_rows[:, mt, j0:j1], in_=res[:, mt, j0:j1])

        for b in range(S // P):
            engine_copy = nc.vector.tensor_copy if b < 2 else nc.scalar.copy
            engine_copy(*pair_views(2, b * P, (b + 1) * P))
        quantize_z(0, P)
        quantize_w2(2, codes2[:])
        quantize_z(P, HALF)
        quantize_w2(3, codes3[:])
        for b in range(2, S // P):
            quantize_z(b * P, (b + 1) * P)
        for mt in (0, 1):
            bank = new_bank(P)
            second_product(bank[:], mt, 0, P)
            empty(res[:, mt, 0:P], bank[:], False)
            store(mt, 0, P)
        for mt in (2, 3):
            bank = new_bank(HALF)
            for b in range(2):
                second_product(bank[:, b * P : (b + 1) * P], mt, b * P, (b + 1) * P)
            empty(res[:, mt, 0:HALF], bank[:], mt == 3)
            store(mt, 0, HALF)
        for mt in (0, 1):
            for j0, j1 in ((P, HALF), (HALF, S)):
                bank = new_bank(j1 - j0)
                second_product(bank[:], mt, j0, j1)
                empty(res[:, mt, j0:j1], bank[:], mt == 0 and j0 == HALF)
            store(mt, P, S)
        bank = new_bank(HALF)
        second_product(bank[:], 2, HALF, S)
        empty(res[:, 2, HALF:S], bank[:], True)
        store(2, HALF, S)
        for b in (2, 3):
            bank = new_bank(P)
            second_product(bank[:], 3, b * P, (b + 1) * P)
            empty(res[:, 3, b * P : (b + 1) * P], bank[:], b == 3)
        store(3, HALF, S)
